import numpy as np
import ml_dtypes


def mxq(x, axis, fmt="e4m3"):
    dtype, down = {"e4m3": (ml_dtypes.float8_e4m3fn, 7), "e5m2": (ml_dtypes.float8_e5m2, 14)}[fmt]
    v = np.moveaxis(np.asarray(x, np.float32).astype(ml_dtypes.bfloat16).astype(np.float64), axis, -1)
    blocks = v.reshape(v.shape[:-1] + (-1, 32))
    amax = np.abs(blocks).max(-1, keepdims=True)
    byte = np.maximum(np.where(amax > 0, np.frexp(amax)[1] - 1 + 127, 0) - down, 1)
    scale = np.exp2(byte - 127.0)
    codes = (blocks / scale).astype(np.float32).astype(dtype).astype(np.float64)
    return np.moveaxis((codes * scale).reshape(v.shape), -1, axis)


WIDE = False


def mx_kscale(k):
    if not WIDE:
        return np.ones(k)
    levels = np.array([18, -18])
    if k % 512:
        return np.exp2(np.random.permutation(np.resize(levels, k // 32))).repeat(32)
    a = np.empty((k // 512, 16))
    for p in range(k // 512):
        a[p, :8] = np.random.permutation(np.resize(levels, 8))
        for g in range(8):
            far = levels[np.abs(levels - a[p, g]) >= 10]
            a[p, g + 8] = far[np.random.randint(len(far))]
    return np.exp2(a.ravel()).repeat(32)


def f64(x):
    return np.asarray(x).astype(np.float64)


def striped(idx):
    return np.tile(np.asarray(idx).reshape(-1, 16).T, (8, 1)).astype(np.uint16)


def unstriped(offs):
    return offs[:16].T.reshape(-1).astype(np.int64)


B, N, T, D, DV, R = 1, 512, 2048, 512, 512, 1024
PAGE = 64


def setup_inputs():
    n = np.random.standard_normal
    pages = np.random.permutation(T // PAGE)[:B * N // PAGE]
    idx = (pages[:, None] * PAGE + np.arange(PAGE)[None, :]).reshape(-1)
    s = mx_kscale(D)[:, None]
    z = mx_kscale(R)[:, None]
    v = mx_kscale(DV)[:, None]
    q = n((B, D, R))
    do = n((B, DV, R))
    return {
        "qT": (q * s).astype(np.float32),
        "kT": (n((D, T)) * (0.50 / np.sqrt(D)) / s).astype(np.float32),
        "vT": (n((DV, T)) / np.sqrt(DV) / v).astype(np.float32),
        "doT": (do * v).astype(np.float32),
        "lse": (np.log(N) + 0.12 + 0.1 * n((B, R, 1))).astype(np.float32),
        "delta": (0.3 * n((B, R, 1))).astype(np.float32),
        "rw": (np.random.uniform(0.5, 1.5, (B, R, 1)) * N / np.sqrt(R) * z).astype(np.float32),
        "qm": (q.transpose(0, 2, 1) / z).astype(np.float32),
        "offs": striped(idx),
    }


def reference(qT, kT, vT, doT, lse, delta, rw, qm, offs):
    idx = unstriped(offs)
    pick = lambda x: x[:, idx].reshape(x.shape[0], B, N).transpose(1, 0, 2)
    a = mxq(f64(qT), 1, "e4m3").transpose(0, 2, 1) @ mxq(pick(f64(kT)), 1, "e4m3")
    p = np.exp(a - f64(lse))
    dp = mxq(f64(doT), 1, "e5m2").transpose(0, 2, 1) @ mxq(pick(f64(vT)), 1, "e4m3")
    ds = f64(rw) * p * (dp - f64(delta))
    dk = mxq(f64(qm), 1, "e4m3").transpose(0, 2, 1) @ mxq(ds, 1, "e5m2")
    gk = np.zeros((D, T))
    gk[:, idx] = dk.transpose(1, 0, 2).reshape(D, B * N)
    return gk

@@ -1,0 +1,259 @@
+from contextlib import ExitStack
+
+import concourse.mybir as mybir
+from concourse.masks import make_identity
+
+N, T, D, DV, R = 512, 2048, 512, 512, 1024
+FLOPS = 2 * R * N * (D + DV + D)
+
+F32 = mybir.dt.float32
+BF16 = mybir.dt.bfloat16
+U32 = mybir.dt.uint32
+U16 = mybir.dt.uint16
+U8 = mybir.dt.uint8
+E4M3 = mybir.dt.float8_e4m3fn_x4
+E5M2 = mybir.dt.float8_e5m2_x4
+ACT = mybir.ActivationFunctionType
+ALU = mybir.AluOpType
+
+P = 128
+PACK = 4
+PASS = P * PACK
+GROUPS = R // PASS
+RUN = 4
+V_SPLIT = 352
+DS_CHUNKS = ((128, 128, 256), (256, 128, 128))
+
+
+def tile_attend_gat_lse_k_kernel(tc, qT, kT, vT, doT, lse, delta, rw, qm, offs, out):
+    nc = tc.nc
+    with ExitStack() as ctx:
+        keep = ctx.enter_context(tc.tile_pool(name="keep", bufs=1))
+        psum = ctx.enter_context(tc.psum_pool(name="psum", bufs=8))
+
+        def bank(name, shape):
+            return psum.tile(shape, F32, name=name, tag="bank")
+
+        def grouped_tile(name):
+            return keep.tile([P, PASS * PACK], BF16, name=name, tag="grouped", bufs=4, align_bytes=64)
+
+        def mx_tiles(name, width):
+            codes = keep.tile([P, width], U32, name=name + "_codes", align_bytes=64)
+            scales = keep.tile([P, width], U8, name=name + "_scales", align_bytes=64)
+            return codes, scales
+
+        def quantize(mx, cols, grouped, fmt):
+            nc.vector.quantize_mx(out=mx[0][:, cols].bitcast(fmt), scales=mx[1][:, cols], in_=grouped)
+
+        def product(acc, lhs, lhs_cols, lhs_fmt, rhs, rhs_fmt, start, stop):
+            nc.tensor.matmul_mx(
+                out=acc[:],
+                lhsT=lhs[0][:, lhs_cols].bitcast(lhs_fmt),
+                lhsT_scale=lhs[1][:, lhs_cols],
+                rhs=rhs[0][:].bitcast(rhs_fmt),
+                rhs_scale=rhs[1][:],
+                start=start,
+                stop=stop,
+            )
+
+        offsets = keep.tile([P, N // 16], U16, name="offsets")
+        nc.sync.dma_start(offsets[:], offs)
+
+        q_raw = keep.tile([P, PACK, R], F32, name="q_raw", tag="query_raw")
+        nc.sync.dma_start(out=q_raw[:], in_=qT[0].rearrange("(p j) r -> p j r", j=PACK))
+
+        stat_rows = keep.tile([P, PASS], F32, name="stat_rows")
+        nc.vector.memset(stat_rows[:], 0.0)
+        for s, vec in enumerate((lse, delta, rw)):
+            nc.sync.dma_start(
+                out=stat_rows[GROUPS * s : GROUPS * (s + 1), :],
+                in_=vec.rearrange("b (g c) o -> (b g) (c o)", g=GROUPS),
+            )
+
+        def load_pool(name, pool):
+            planes = []
+            for j in range(PACK):
+                plane = keep.tile([P, T], F32, name="%s_plane%d" % (name, j))
+                nc.sync.dma_start(out=plane[:], in_=pool.rearrange("(p j) t -> p j t", j=PACK)[:, j, :])
+                planes.append(plane)
+            return planes
+
+        k_planes = load_pool("k", kT)
+        v_planes = load_pool("v", vT)
+
+        half = PASS // 2
+        do_raw = []
+        for h in range(2 * GROUPS):
+            piece = keep.tile([P, PACK, half], F32, name="do_raw%d" % h)
+            nc.sync.dma_start(out=piece[:], in_=doT[0].rearrange("(p j) r -> p j r", j=PACK)[:, :, h * half : (h + 1) * half])
+            do_raw.append(piece)
+
+        windows = []
+        for k in range(D // P):
+            window = keep.tile([P, T], F32, name="window%d" % k)
+            nc.vector.memset(window[:], 0.0)
+            windows.append(window)
+
+        ident = keep.tile([P, P], F32, name="ident")
+        make_identity(nc, ident[:])
+        stat_bank = bank("stat_bank", [P, PACK, P])
+        for t in range(PACK):
+            nc.tensor.transpose(stat_bank[:, t, :], stat_rows[:, t:PASS:PACK], ident[:])
+        stats = keep.tile([P, PACK, 8], F32, name="stats")
+        nc.vector.tensor_copy(out=stats[:], in_=stat_bank[:, :, 0:8])
+        neg_lse = keep.tile([P, PACK, GROUPS], F32, name="neg_lse")
+        nc.vector.tensor_scalar(out=neg_lse[:], in0=stats[:, :, 0:2], scalar1=-1.0, scalar2=None, op0=ALU.mult)
+        neg_delta_rw = keep.tile([P, PACK, GROUPS], F32, name="neg_delta_rw")
+        nc.vector.scalar_tensor_tensor(
+            out=neg_delta_rw[:], in0=stats[:, :, 2:4], scalar=-1.0, in1=stats[:, :, 4:6], op0=ALU.mult, op1=ALU.mult
+        )
+
+        q_mx = [mx_tiles("q%d" % g, PASS) for g in range(GROUPS)]
+        q_grouped = []
+        for g in range(GROUPS):
+            grouped = grouped_tile("q_grouped%d" % g)
+            nc.vector.tensor_copy(
+                out=grouped[:].rearrange("p (t m j) -> p m j t", t=PACK, j=PACK),
+                in_=q_raw[:, :, g * PASS : (g + 1) * PASS].rearrange("p j (m t) -> p m j t", t=PACK),
+            )
+            q_grouped.append(grouped)
+        for g in range(GROUPS):
+            quantize(q_mx[g], slice(0, PASS), q_grouped[g][:], E4M3)
+
+        qm_raw = keep.tile([P, GROUPS, PACK, D], F32, name="qm_raw", tag="query_raw")
+        for g in range(GROUPS):
+            nc.sync.dma_start(
+                out=qm_raw[:, g, :, :], in_=qm[0, g * PASS : (g + 1) * PASS, :].rearrange("(p t) d -> p t d", t=PACK)
+            )
+
+        def interleave(engine_copy, grouped, planes, lo, hi):
+            engine_copy(
+                out=grouped[:, lo * PACK : hi * PACK].rearrange("p (c x j) -> p c j x", x=RUN, j=PACK),
+                in_=planes[:, :, lo:hi].rearrange("p j (c x) -> p c j x", x=RUN),
+            )
+
+        def gather_pool(name, planes, split):
+            picked = keep.tile([P, PACK, N], F32, name=name + "_picked", tag="picked")
+            for j in range(PACK):
+                nc.vector.tensor_copy(picked[:, j, :], planes[j][:].indirect(offsets[:]))
+            grouped = grouped_tile(name + "_grouped")
+            interleave(nc.vector.tensor_copy, grouped, picked, 0, split)
+            if split < N:
+                interleave(nc.scalar.copy, grouped, picked, split, N)
+            mx = mx_tiles(name, N)
+            quantize(mx, slice(0, N), grouped[:], E4M3)
+            return mx
+
+        k_mx = gather_pool("k", k_planes, N)
+        weights = []
+        for g in range(GROUPS):
+            p_g = keep.tile([P, PACK, N], F32, name="weights%d" % g)
+            for t in range(PACK):
+                acc = bank("score", [P, N])
+                product(acc, q_mx[g], slice(t * P, (t + 1) * P), E4M3, k_mx, E4M3, True, True)
+                nc.scalar.activation(out=p_g[:, t, :], in_=acc[:], func=ACT.Exp, bias=neg_lse[:, t, g : g + 1], scale=1.0)
+            weights.append(p_g)
+
+        v_mx = gather_pool("v", v_planes, V_SPLIT)
+
+        do_mx = [mx_tiles("do%d" % g, PASS) for g in range(GROUPS)]
+        ds_mx = [mx_tiles("ds%d" % g, N) for g in range(GROUPS)]
+        do_grouped = [None] * GROUPS
+
+        def group_do(h, engine_copy, t0, t1):
+            g, part = divmod(h, 2)
+            if do_grouped[g] is None:
+                do_grouped[g] = grouped_tile("do_grouped%d" % g)
+            m0 = part * (P // 2)
+            engine_copy(
+                out=do_grouped[g][:].rearrange("p (t m j) -> p m j t", t=PACK, j=PACK)[:, m0 : m0 + P // 2, :, t0:t1],
+                in_=do_raw[h][:].rearrange("p j (m t) -> p m j t", t=PACK)[:, :, :, t0:t1],
+            )
+
+        def grad_products(g):
+            accs = []
+            for t in range(PACK):
+                cols = slice(t * P, (t + 1) * P)
+                quantize(do_mx[g], cols, do_grouped[g][:, t * PASS : (t + 1) * PASS], E5M2)
+                acc = bank("dp", [P, N])
+                product(acc, do_mx[g], cols, E5M2, v_mx, E4M3, True, True)
+                accs.append(acc)
+            return accs
+
+        def ds_steps(g, accs):
+            centred = keep.tile([P, PACK, N], F32, name="centred%d" % g)
+            grouped = grouped_tile("ds_grouped%d" % g)
+            steps = []
+            lo = 0
+            for width in DS_CHUNKS[g]:
+                steps.append((g, accs, centred, grouped, lo, lo + width))
+                lo += width
+            return steps
+
+        def centre(step):
+            g, accs, centred, grouped, lo, hi = step
+            for t in range(PACK):
+                nc.scalar.activation(
+                    out=centred[:, t, lo:hi], in_=accs[t][:, lo:hi], func=ACT.Identity,
+                    bias=neg_delta_rw[:, t, g : g + 1], scale=stats[:, t, 4 + g : 5 + g],
+                )
+
+        def multiply(step):
+            g, accs, centred, grouped, lo, hi = step
+            nc.vector.tensor_tensor(
+                out=grouped[:, lo * PACK : hi * PACK].rearrange("p (c x t) -> p c t x", x=RUN, t=PACK),
+                in0=weights[g][:, :, lo:hi].rearrange("p t (c x) -> p c t x", x=RUN),
+                in1=centred[:, :, lo:hi].rearrange("p t (c x) -> p c t x", x=RUN),
+                op=ALU.mult,
+            )
+
+        def quantize_ds(step):
+            g, accs, centred, grouped, lo, hi = step
+            quantize(ds_mx[g], slice(lo, hi), grouped[:, lo * PACK : hi * PACK], E5M2)
+
+        qm_mx = [mx_tiles("qm%d" % k, GROUPS * P) for k in range(D // P)]
+        qm_grouped = [
+            keep.tile([P, GROUPS, P * PACK], BF16, name="qm_grouped%d" % k, align_bytes=64) for k in range(D // P)
+        ]
+
+        def group_qm(k, engine_copy):
+            for g in range(GROUPS):
+                engine_copy(
+                    out=qm_grouped[k][:, g, :].rearrange("p (c x t) -> p c t x", x=RUN, t=PACK),
+                    in_=qm_raw[:, g, :, k * P : (k + 1) * P].rearrange("p t (c x) -> p c t x", x=RUN),
+                )
+
+        def quantize_qm(k):
+            quantize(qm_mx[k], slice(0, GROUPS * P), qm_grouped[k][:].rearrange("p g w -> p (g w)"), E4M3)
+
+        group_do(0, nc.vector.tensor_copy, 0, PACK)
+        group_do(1, nc.vector.tensor_copy, 0, 2)
+        group_do(1, nc.scalar.copy, 2, PACK)
+        steps0 = ds_steps(0, grad_products(0))
+        for step in steps0:
+            centre(step)
+        group_do(2, nc.vector.tensor_copy, 0, PACK)
+        group_do(3, nc.vector.tensor_copy, 0, PACK)
+        steps1 = ds_steps(1, grad_products(1))
+        for step in steps1:
+            centre(step)
+        group_qm(0, nc.scalar.copy)
+        steps = steps0 + steps1
+        for s, step in enumerate(steps):
+            multiply(step)
+            if s > 0:
+                quantize_ds(steps[s - 1])
+        quantize_qm(0)
+        quantize_ds(steps[-1])
+
+        for k in range(D // P):
+            acc = bank("grad", [P, N])
+            for g in range(GROUPS):
+                product(acc, qm_mx[k], slice(g * P, (g + 1) * P), E4M3, ds_mx[g], E5M2, g == 0, g == GROUPS - 1)
+            staged = keep.tile([P, N], F32, name="staged", bufs=2)
+            nc.scalar.copy(out=staged[:], in_=acc[:])
+            nc.vector.tensor_copy(windows[k][:].indirect(offsets[:]), staged[:])
+            nc.sync.dma_start(out=out[k * P : (k + 1) * P, :], in_=windows[k][:])
+            if k + 1 < D // P:
+                group_qm(k + 1, nc.scalar.copy)
+                quantize_qm(k + 1)

@@ -22,7 +22,9 @@ PASS = P * PACK
 GROUPS = R // PASS
 RUN = 4
 V_SPLIT = 352
-DS_CHUNKS = ((128, 128, 256), (256, 128, 128))
+WARM_PASSES = 5
+DO_PIECES = ((0, 512), (512, 768), (768, 1024))
+DS_CHUNKS = ((256, 256), (256, 256))
 
 
 def tile_attend_gat_lse_k_kernel(tc, qT, kT, vT, doT, lse, delta, rw, qm, offs, out):
@@ -59,17 +61,6 @@ def tile_attend_gat_lse_k_kernel(tc, qT, kT, vT, doT, lse, delta, rw, qm, offs, 
         offsets = keep.tile([P, N // 16], U16, name="offsets")
         nc.sync.dma_start(offsets[:], offs)
 
-        q_raw = keep.tile([P, PACK, R], F32, name="q_raw", tag="query_raw")
-        nc.sync.dma_start(out=q_raw[:], in_=qT[0].rearrange("(p j) r -> p j r", j=PACK))
-
-        stat_rows = keep.tile([P, PASS], F32, name="stat_rows")
-        nc.vector.memset(stat_rows[:], 0.0)
-        for s, vec in enumerate((lse, delta, rw)):
-            nc.sync.dma_start(
-                out=stat_rows[GROUPS * s : GROUPS * (s + 1), :],
-                in_=vec.rearrange("b (g c) o -> (b g) (c o)", g=GROUPS),
-            )
-
         def load_pool(name, pool):
             planes = []
             for j in range(PACK):
@@ -79,19 +70,29 @@ def tile_attend_gat_lse_k_kernel(tc, qT, kT, vT, doT, lse, delta, rw, qm, offs, 
             return planes
 
         k_planes = load_pool("k", kT)
+        stat_rows = keep.tile([P, PASS], F32, name="stat_rows")
+        nc.vector.memset(stat_rows[:], 0.0)
+        for s, vec in enumerate((lse, delta, rw)):
+            nc.sync.dma_start(
+                out=stat_rows[GROUPS * s : GROUPS * (s + 1), :],
+                in_=vec.rearrange("b (g c) o -> (b g) (c o)", g=GROUPS),
+            )
+
+        q_raw = keep.tile([P, PACK, R], F32, name="q_raw", tag="query_raw")
+        nc.sync.dma_start(out=q_raw[:], in_=qT[0].rearrange("(p j) r -> p j r", j=PACK))
+
         v_planes = load_pool("v", vT)
 
-        half = PASS // 2
         do_raw = []
-        for h in range(2 * GROUPS):
-            piece = keep.tile([P, PACK, half], F32, name="do_raw%d" % h)
-            nc.sync.dma_start(out=piece[:], in_=doT[0].rearrange("(p j) r -> p j r", j=PACK)[:, :, h * half : (h + 1) * half])
+        for lo, hi in DO_PIECES:
+            piece = keep.tile([P, PACK, hi - lo], F32, name="do_raw%d" % lo)
+            nc.sync.dma_start(out=piece[:], in_=doT[0].rearrange("(p j) r -> p j r", j=PACK)[:, :, lo:hi])
             do_raw.append(piece)
 
         windows = []
         for k in range(D // P):
             window = keep.tile([P, T], F32, name="window%d" % k)
-            nc.vector.memset(window[:], 0.0)
+            (nc.vector if k == 0 else nc.gpsimd).memset(window[:], 0.0)
             windows.append(window)
 
         ident = keep.tile([P, P], F32, name="ident")
@@ -107,24 +108,6 @@ def tile_attend_gat_lse_k_kernel(tc, qT, kT, vT, doT, lse, delta, rw, qm, offs, 
         nc.vector.scalar_tensor_tensor(
             out=neg_delta_rw[:], in0=stats[:, :, 2:4], scalar=-1.0, in1=stats[:, :, 4:6], op0=ALU.mult, op1=ALU.mult
         )
-
-        q_mx = [mx_tiles("q%d" % g, PASS) for g in range(GROUPS)]
-        q_grouped = []
-        for g in range(GROUPS):
-            grouped = grouped_tile("q_grouped%d" % g)
-            nc.vector.tensor_copy(
-                out=grouped[:].rearrange("p (t m j) -> p m j t", t=PACK, j=PACK),
-                in_=q_raw[:, :, g * PASS : (g + 1) * PASS].rearrange("p j (m t) -> p m j t", t=PACK),
-            )
-            q_grouped.append(grouped)
-        for g in range(GROUPS):
-            quantize(q_mx[g], slice(0, PASS), q_grouped[g][:], E4M3)
-
-        qm_raw = keep.tile([P, GROUPS, PACK, D], F32, name="qm_raw", tag="query_raw")
-        for g in range(GROUPS):
-            nc.sync.dma_start(
-                out=qm_raw[:, g, :, :], in_=qm[0, g * PASS : (g + 1) * PASS, :].rearrange("(p t) d -> p t d", t=PACK)
-            )
 
         def interleave(engine_copy, grouped, planes, lo, hi):
             engine_copy(
@@ -142,9 +125,24 @@ def tile_attend_gat_lse_k_kernel(tc, qT, kT, vT, doT, lse, delta, rw, qm, offs, 
                 interleave(nc.scalar.copy, grouped, picked, split, N)
             mx = mx_tiles(name, N)
             quantize(mx, slice(0, N), grouped[:], E4M3)
-            return mx
+            return mx, picked
 
-        k_mx = gather_pool("k", k_planes, N)
+        k_mx, k_picked = gather_pool("k", k_planes, N)
+        q_mx = [mx_tiles("q%d" % g, PASS) for g in range(GROUPS)]
+        for g in range(GROUPS):
+            grouped = grouped_tile("q_grouped%d" % g)
+            nc.vector.tensor_copy(
+                out=grouped[:].rearrange("p (t m j) -> p m j t", t=PACK, j=PACK),
+                in_=q_raw[:, :, g * PASS : (g + 1) * PASS].rearrange("p j (m t) -> p m j t", t=PACK),
+            )
+            quantize(q_mx[g], slice(0, PASS), grouped[:], E4M3)
+
+        qm_raw = keep.tile([P, GROUPS, PACK, D], F32, name="qm_raw", tag="query_raw")
+        for g in range(GROUPS):
+            nc.sync.dma_start(
+                out=qm_raw[:, g, :, :], in_=qm[0, g * PASS : (g + 1) * PASS, :].rearrange("(p t) d -> p t d", t=PACK)
+            )
+
         weights = []
         for g in range(GROUPS):
             p_g = keep.tile([P, PACK, N], F32, name="weights%d" % g)
@@ -154,27 +152,35 @@ def tile_attend_gat_lse_k_kernel(tc, qT, kT, vT, doT, lse, delta, rw, qm, offs, 
                 nc.scalar.activation(out=p_g[:, t, :], in_=acc[:], func=ACT.Exp, bias=neg_lse[:, t, g : g + 1], scale=1.0)
             weights.append(p_g)
 
-        v_mx = gather_pool("v", v_planes, V_SPLIT)
+        v_mx, v_picked = gather_pool("v", v_planes, V_SPLIT)
+        warm = bank("warm", [P, N])
+        nc.tensor.transpose(warm[:, 0:P], v_picked[:, PACK - 1, 0:P], ident[:])
+        for w in range(WARM_PASSES):
+            product(warm, q_mx[0], slice(0, P), E4M3, k_mx, E4M3, True, True)
 
         do_mx = [mx_tiles("do%d" % g, PASS) for g in range(GROUPS)]
         ds_mx = [mx_tiles("ds%d" % g, N) for g in range(GROUPS)]
         do_grouped = [None] * GROUPS
 
         def group_do(h, engine_copy, t0, t1):
-            g, part = divmod(h, 2)
+            lo, hi = DO_PIECES[h]
+            g = lo // PASS
             if do_grouped[g] is None:
                 do_grouped[g] = grouped_tile("do_grouped%d" % g)
-            m0 = part * (P // 2)
+            m0, m1 = (lo - g * PASS) // PACK, (hi - g * PASS) // PACK
             engine_copy(
-                out=do_grouped[g][:].rearrange("p (t m j) -> p m j t", t=PACK, j=PACK)[:, m0 : m0 + P // 2, :, t0:t1],
+                out=do_grouped[g][:].rearrange("p (t m j) -> p m j t", t=PACK, j=PACK)[:, m0:m1, :, t0:t1],
                 in_=do_raw[h][:].rearrange("p j (m t) -> p m j t", t=PACK)[:, :, :, t0:t1],
             )
 
-        def grad_products(g):
+        def grad_products(g, span):
             accs = []
             for t in range(PACK):
                 cols = slice(t * P, (t + 1) * P)
-                quantize(do_mx[g], cols, do_grouped[g][:, t * PASS : (t + 1) * PASS], E5M2)
+                if t % span == 0:
+                    quantize(
+                        do_mx[g], slice(t * P, (t + span) * P), do_grouped[g][:, t * PASS : (t + span) * PASS], E5M2
+                    )
                 acc = bank("dp", [P, N])
                 product(acc, do_mx[g], cols, E5M2, v_mx, E4M3, True, True)
                 accs.append(acc)
@@ -182,10 +188,10 @@ def tile_attend_gat_lse_k_kernel(tc, qT, kT, vT, doT, lse, delta, rw, qm, offs, 
 
         def ds_steps(g, accs):
             centred = keep.tile([P, PACK, N], F32, name="centred%d" % g)
-            grouped = grouped_tile("ds_grouped%d" % g)
             steps = []
             lo = 0
             for width in DS_CHUNKS[g]:
+                grouped = keep.tile([P, width * PACK], BF16, name="ds_grouped%d_%d" % (g, lo), align_bytes=64)
                 steps.append((g, accs, centred, grouped, lo, lo + width))
                 lo += width
             return steps
@@ -201,7 +207,7 @@ def tile_attend_gat_lse_k_kernel(tc, qT, kT, vT, doT, lse, delta, rw, qm, offs, 
         def multiply(step):
             g, accs, centred, grouped, lo, hi = step
             nc.vector.tensor_tensor(
-                out=grouped[:, lo * PACK : hi * PACK].rearrange("p (c x t) -> p c t x", x=RUN, t=PACK),
+                out=grouped[:].rearrange("p (c x t) -> p c t x", x=RUN, t=PACK),
                 in0=weights[g][:, :, lo:hi].rearrange("p t (c x) -> p c t x", x=RUN),
                 in1=centred[:, :, lo:hi].rearrange("p t (c x) -> p c t x", x=RUN),
                 op=ALU.mult,
@@ -209,51 +215,66 @@ def tile_attend_gat_lse_k_kernel(tc, qT, kT, vT, doT, lse, delta, rw, qm, offs, 
 
         def quantize_ds(step):
             g, accs, centred, grouped, lo, hi = step
-            quantize(ds_mx[g], slice(lo, hi), grouped[:, lo * PACK : hi * PACK], E5M2)
+            quantize(ds_mx[g], slice(lo, hi), grouped[:], E5M2)
 
-        qm_mx = [mx_tiles("qm%d" % k, GROUPS * P) for k in range(D // P)]
-        qm_grouped = [
-            keep.tile([P, GROUPS, P * PACK], BF16, name="qm_grouped%d" % k, align_bytes=64) for k in range(D // P)
-        ]
+        qm_mx = [None] * (D // P)
+        qm_grouped = [None] * (D // P)
 
-        def group_qm(k, engine_copy):
+        def group_qm(k, engine_copy, tag):
+            qm_grouped[k] = keep.tile([P, GROUPS, P * PACK], BF16, name="qm_grouped%d" % k, tag=tag, align_bytes=64)
             for g in range(GROUPS):
                 engine_copy(
                     out=qm_grouped[k][:, g, :].rearrange("p (c x t) -> p c t x", x=RUN, t=PACK),
                     in_=qm_raw[:, g, :, k * P : (k + 1) * P].rearrange("p t (c x) -> p c t x", x=RUN),
                 )
 
-        def quantize_qm(k):
+        def quantize_qm(k, tag):
+            codes = keep.tile([P, GROUPS * P], U32, name="qm%d_codes" % k, tag=tag, align_bytes=64)
+            scales = keep.tile([P, GROUPS * P], U8, name="qm%d_scales" % k, align_bytes=64)
+            qm_mx[k] = (codes, scales)
             quantize(qm_mx[k], slice(0, GROUPS * P), qm_grouped[k][:].rearrange("p g w -> p (g w)"), E4M3)
 
-        group_do(0, nc.vector.tensor_copy, 0, PACK)
-        group_do(1, nc.vector.tensor_copy, 0, 2)
-        group_do(1, nc.scalar.copy, 2, PACK)
-        steps0 = ds_steps(0, grad_products(0))
+        group_do(0, nc.vector.tensor_copy, 0, 2)
+        group_do(0, nc.scalar.copy, 2, PACK)
+        group_do(1, nc.scalar.copy, 0, PACK)
+        steps0 = ds_steps(0, grad_products(0, 2))
         for step in steps0:
             centre(step)
-        group_do(2, nc.vector.tensor_copy, 0, PACK)
-        group_do(3, nc.vector.tensor_copy, 0, PACK)
-        steps1 = ds_steps(1, grad_products(1))
+        group_do(2, nc.vector.tensor_copy, 0, 2)
+        group_do(2, nc.vector.tensor_copy, 2, PACK)
+        steps1 = ds_steps(1, grad_products(1, 2))
         for step in steps1:
             centre(step)
-        group_qm(0, nc.scalar.copy)
+        group_qm(0, nc.scalar.copy, "qm_grouped0")
         steps = steps0 + steps1
         for s, step in enumerate(steps):
             multiply(step)
             if s > 0:
                 quantize_ds(steps[s - 1])
-        quantize_qm(0)
+        quantize_qm(0, "qm0_codes")
         quantize_ds(steps[-1])
 
-        for k in range(D // P):
+        def finish(k, parts):
             acc = bank("grad", [P, N])
             for g in range(GROUPS):
                 product(acc, qm_mx[k], slice(g * P, (g + 1) * P), E4M3, ds_mx[g], E5M2, g == 0, g == GROUPS - 1)
-            staged = keep.tile([P, N], F32, name="staged", bufs=2)
-            nc.scalar.copy(out=staged[:], in_=acc[:])
-            nc.vector.tensor_copy(windows[k][:].indirect(offsets[:]), staged[:])
+            staged = keep.tile([P, N], F32, name="staged%d" % k, align_bytes=64)
+            width = N // parts
+            for part in range(parts):
+                cols = slice(part * width, (part + 1) * width)
+                nc.scalar.copy(out=staged[:, cols], in_=acc[:, cols])
+                nc.vector.tensor_copy(
+                    windows[k][:].indirect(offsets[:, part * width // 16 : (part + 1) * width // 16]), staged[:, cols]
+                )
             nc.sync.dma_start(out=out[k * P : (k + 1) * P, :], in_=windows[k][:])
-            if k + 1 < D // P:
-                group_qm(k + 1, nc.scalar.copy)
-                quantize_qm(k + 1)
+
+        finish(0, 2)
+        group_qm(1, nc.scalar.copy, "qm_grouped1")
+        quantize_qm(1, "ds_grouped1_0")
+        finish(1, 1)
+        group_qm(2, nc.vector.tensor_copy, "ds_grouped1_256")
+        quantize_qm(2, "qm2_codes")
+        finish(2, 1)
+        group_qm(3, nc.scalar.copy, "staged0")
+        quantize_qm(3, "qm3_codes")
+        finish(3, 1)

@@ -61,15 +61,15 @@ def tile_attend_gat_lse_k_kernel(tc, qT, kT, vT, doT, lse, delta, rw, qm, offs, 
         offsets = keep.tile([P, N // 16], U16, name="offsets")
         nc.sync.dma_start(offsets[:], offs)
 
-        def load_pool(name, pool):
+        def load_pool(name, pool, runs):
             planes = []
-            for j in range(PACK):
-                plane = keep.tile([P, T], F32, name="%s_plane%d" % (name, j))
-                nc.sync.dma_start(out=plane[:], in_=pool.rearrange("(p j) t -> p j t", j=PACK)[:, j, :])
-                planes.append(plane)
+            for lo, hi in runs:
+                piece = keep.tile([P, hi - lo, T], F32, name="%s_planes%d" % (name, lo))
+                nc.sync.dma_start(out=piece[:], in_=pool.rearrange("(p j) t -> p j t", j=PACK)[:, lo:hi, :])
+                planes.extend(piece[:, j, :] for j in range(hi - lo))
             return planes
 
-        k_planes = load_pool("k", kT)
+        k_planes = load_pool("k", kT, ((0, 2), (2, PACK)))
         stat_rows = keep.tile([P, PASS], F32, name="stat_rows")
         nc.vector.memset(stat_rows[:], 0.0)
         for s, vec in enumerate((lse, delta, rw)):
@@ -81,7 +81,7 @@ def tile_attend_gat_lse_k_kernel(tc, qT, kT, vT, doT, lse, delta, rw, qm, offs, 
         q_raw = keep.tile([P, PACK, R], F32, name="q_raw", tag="query_raw")
         nc.sync.dma_start(out=q_raw[:], in_=qT[0].rearrange("(p j) r -> p j r", j=PACK))
 
-        v_planes = load_pool("v", vT)
+        v_planes = load_pool("v", vT, ((0, 2), (2, 3), (3, PACK)))
 
         do_raw = []
         for lo, hi in DO_PIECES:
@@ -109,20 +109,24 @@ def tile_attend_gat_lse_k_kernel(tc, qT, kT, vT, doT, lse, delta, rw, qm, offs, 
             out=neg_delta_rw[:], in0=stats[:, :, 2:4], scalar=-1.0, in1=stats[:, :, 4:6], op0=ALU.mult, op1=ALU.mult
         )
 
-        def interleave(engine_copy, grouped, planes, lo, hi):
+        def interleave(engine_copy, grouped, planes, lo, hi, j0, j1):
             engine_copy(
-                out=grouped[:, lo * PACK : hi * PACK].rearrange("p (c x j) -> p c j x", x=RUN, j=PACK),
-                in_=planes[:, :, lo:hi].rearrange("p j (c x) -> p c j x", x=RUN),
+                out=grouped[:, lo * PACK : hi * PACK].rearrange("p (c x j) -> p c j x", x=RUN, j=PACK)[:, :, j0:j1, :],
+                in_=planes[:, j0:j1, lo:hi].rearrange("p j (c x) -> p c j x", x=RUN),
             )
 
         def gather_pool(name, planes, split):
             picked = keep.tile([P, PACK, N], F32, name=name + "_picked", tag="picked")
-            for j in range(PACK):
-                nc.vector.tensor_copy(picked[:, j, :], planes[j][:].indirect(offsets[:]))
             grouped = grouped_tile(name + "_grouped")
-            interleave(nc.vector.tensor_copy, grouped, picked, 0, split)
+            for j in range(PACK):
+                nc.vector.tensor_copy(picked[:, j, :], planes[j].indirect(offsets[:]))
+                if split < N and j == 1:
+                    interleave(nc.vector.tensor_copy, grouped, picked, 0, N, 0, 2)
             if split < N:
-                interleave(nc.scalar.copy, grouped, picked, split, N)
+                interleave(nc.vector.tensor_copy, grouped, picked, 0, split, 2, PACK)
+                interleave(nc.scalar.copy, grouped, picked, split, N, 2, PACK)
+            else:
+                interleave(nc.vector.tensor_copy, grouped, picked, 0, N, 0, PACK)
             mx = mx_tiles(name, N)
             quantize(mx, slice(0, N), grouped[:], E4M3)
             return mx, picked
@@ -249,9 +253,10 @@ def tile_attend_gat_lse_k_kernel(tc, qT, kT, vT, doT, lse, delta, rw, qm, offs, 
         steps = steps0 + steps1
         for s, step in enumerate(steps):
             multiply(step)
+            if s == len(steps) - 1:
+                quantize_qm(0, "qm0_codes")
             if s > 0:
                 quantize_ds(steps[s - 1])
-        quantize_qm(0, "qm0_codes")
         quantize_ds(steps[-1])
 
         def finish(k, parts):

@@ -135,10 +135,11 @@ def tile_attend_gat_lse_k_kernel(tc, qT, kT, vT, doT, lse, delta, rw, qm, offs, 
         q_mx = [mx_tiles("q%d" % g, PASS) for g in range(GROUPS)]
         for g in range(GROUPS):
             grouped = grouped_tile("q_grouped%d" % g)
-            nc.vector.tensor_copy(
-                out=grouped[:].rearrange("p (t m j) -> p m j t", t=PACK, j=PACK),
-                in_=q_raw[:, :, g * PASS : (g + 1) * PASS].rearrange("p j (m t) -> p m j t", t=PACK),
-            )
+            for t0 in (0, 2):
+                nc.vector.tensor_copy(
+                    out=grouped[:].rearrange("p (t m j) -> p m j t", t=PACK, j=PACK)[:, :, :, t0 : t0 + 2],
+                    in_=q_raw[:, :, g * PASS : (g + 1) * PASS].rearrange("p j (m t) -> p m j t", t=PACK)[:, :, :, t0 : t0 + 2],
+                )
             quantize(q_mx[g], slice(0, PASS), grouped[:], E4M3)
 
         qm_raw = keep.tile([P, GROUPS, PACK, D], F32, name="qm_raw", tag="query_raw")
@@ -191,10 +192,10 @@ def tile_attend_gat_lse_k_kernel(tc, qT, kT, vT, doT, lse, delta, rw, qm, offs, 
             return accs
 
         def ds_steps(g, accs):
-            centred = keep.tile([P, PACK, N], F32, name="centred%d" % g)
             steps = []
             lo = 0
             for width in DS_CHUNKS[g]:
+                centred = keep.tile([P, PACK, width], F32, name="centred%d_%d" % (g, lo))
                 grouped = keep.tile([P, width * PACK], BF16, name="ds_grouped%d_%d" % (g, lo), align_bytes=64)
                 steps.append((g, accs, centred, grouped, lo, lo + width))
                 lo += width
@@ -204,16 +205,16 @@ def tile_attend_gat_lse_k_kernel(tc, qT, kT, vT, doT, lse, delta, rw, qm, offs, 
             g, accs, centred, grouped, lo, hi = step
             for t in range(PACK):
                 nc.scalar.activation(
-                    out=centred[:, t, lo:hi], in_=accs[t][:, lo:hi], func=ACT.Identity,
+                    out=centred[:, t, :], in_=accs[t][:, lo:hi], func=ACT.Identity,
                     bias=neg_delta_rw[:, t, g : g + 1], scale=stats[:, t, 4 + g : 5 + g],
                 )
 
         def multiply(step):
             g, accs, centred, grouped, lo, hi = step
             nc.vector.tensor_tensor(
-                out=grouped[:].rearrange("p (c x t) -> p c t x", x=RUN, t=PACK),
-                in0=weights[g][:, :, lo:hi].rearrange("p t (c x) -> p c t x", x=RUN),
-                in1=centred[:, :, lo:hi].rearrange("p t (c x) -> p c t x", x=RUN),
+                out=grouped[:].rearrange("p (c x t) -> p c t x", x=2, t=PACK),
+                in0=weights[g][:, :, lo:hi].rearrange("p t (c x) -> p c t x", x=2),
+                in1=centred[:].rearrange("p t (c x) -> p c t x", x=2),
                 op=ALU.mult,
             )
 
@@ -240,7 +241,8 @@ def tile_attend_gat_lse_k_kernel(tc, qT, kT, vT, doT, lse, delta, rw, qm, offs, 
 
         group_do(0, nc.vector.tensor_copy, 0, 2)
         group_do(0, nc.scalar.copy, 2, PACK)
-        group_do(1, nc.scalar.copy, 0, PACK)
+        group_do(1, nc.scalar.copy, 0, 2)
+        group_do(1, nc.scalar.copy, 2, PACK)
         steps0 = ds_steps(0, grad_products(0, 2))
         for step in steps0:
             centre(step)
@@ -263,23 +265,22 @@ def tile_attend_gat_lse_k_kernel(tc, qT, kT, vT, doT, lse, delta, rw, qm, offs, 
             acc = bank("grad", [P, N])
             for g in range(GROUPS):
                 product(acc, qm_mx[k], slice(g * P, (g + 1) * P), E4M3, ds_mx[g], E5M2, g == 0, g == GROUPS - 1)
-            staged = keep.tile([P, N], F32, name="staged%d" % k, align_bytes=64)
             width = N // parts
             for part in range(parts):
-                cols = slice(part * width, (part + 1) * width)
-                nc.scalar.copy(out=staged[:, cols], in_=acc[:, cols])
+                staged = keep.tile([P, width], F32, name="staged%d_%d" % (k, part), align_bytes=64)
+                nc.scalar.copy(out=staged[:], in_=acc[:, part * width : (part + 1) * width])
                 nc.vector.tensor_copy(
-                    windows[k][:].indirect(offsets[:, part * width // 16 : (part + 1) * width // 16]), staged[:, cols]
+                    windows[k][:].indirect(offsets[:, part * width // 16 : (part + 1) * width // 16]), staged[:]
                 )
             nc.sync.dma_start(out=out[k * P : (k + 1) * P, :], in_=windows[k][:])
 
-        finish(0, 2)
+        finish(0, 1)
         group_qm(1, nc.scalar.copy, "qm_grouped1")
         quantize_qm(1, "ds_grouped1_0")
         finish(1, 1)
         group_qm(2, nc.vector.tensor_copy, "ds_grouped1_256")
         quantize_qm(2, "qm2_codes")
         finish(2, 1)
-        group_qm(3, nc.scalar.copy, "staged0")
-        quantize_qm(3, "qm3_codes")
+        group_qm(3, nc.scalar.copy, "qm_grouped3")
+        quantize_qm(3, "staged0_0")
         finish(3, 1)

@@ -20,15 +20,14 @@ P = 128
 PACK = 4
 PASS = P * PACK
 GROUPS = R // PASS
+HALF = N // 2
 RUN = 4
-V_SPLIT = 352
-WARM_PASSES = 5
-DO_PIECES = ((0, 512), (512, 768), (768, 1024))
-DS_CHUNKS = ((256, 256), (256, 256))
+WARM_PASSES = 2
 
 
 def tile_attend_gat_lse_k_kernel(tc, qT, kT, vT, doT, lse, delta, rw, qm, offs, out):
     nc = tc.nc
+    vcopy, scopy = nc.vector.tensor_copy, nc.scalar.copy
     with ExitStack() as ctx:
         keep = ctx.enter_context(tc.tile_pool(name="keep", bufs=1))
         psum = ctx.enter_context(tc.psum_pool(name="psum", bufs=8))
@@ -36,24 +35,22 @@ def tile_attend_gat_lse_k_kernel(tc, qT, kT, vT, doT, lse, delta, rw, qm, offs, 
         def bank(name, shape):
             return psum.tile(shape, F32, name=name, tag="bank")
 
-        def grouped_tile(name):
-            return keep.tile([P, PASS * PACK], BF16, name=name, tag="grouped", bufs=4, align_bytes=64)
+        def sb(name, shape, dtype, tag=None):
+            return keep.tile(shape, dtype, name=name, tag=tag or name, align_bytes=64)
 
-        def mx_tiles(name, width):
-            codes = keep.tile([P, width], U32, name=name + "_codes", align_bytes=64)
-            scales = keep.tile([P, width], U8, name=name + "_scales", align_bytes=64)
-            return codes, scales
+        def mx_tiles(name, width, tag=None):
+            return sb(name + "_codes", [P, width], U32, tag), sb(name + "_scales", [P, width], U8)
 
-        def quantize(mx, cols, grouped, fmt):
-            nc.vector.quantize_mx(out=mx[0][:, cols].bitcast(fmt), scales=mx[1][:, cols], in_=grouped)
+        def quantize(mx, lo, hi, grouped, fmt):
+            nc.vector.quantize_mx(out=mx[0][:, lo:hi].bitcast(fmt), scales=mx[1][:, lo:hi], in_=grouped)
 
-        def product(acc, lhs, lhs_cols, lhs_fmt, rhs, rhs_fmt, start, stop):
+        def product(acc, lhs, lhs_lo, lhs_fmt, rhs, rhs_lo, rhs_hi, rhs_fmt, start=True, stop=True):
             nc.tensor.matmul_mx(
-                out=acc[:],
-                lhsT=lhs[0][:, lhs_cols].bitcast(lhs_fmt),
-                lhsT_scale=lhs[1][:, lhs_cols],
-                rhs=rhs[0][:].bitcast(rhs_fmt),
-                rhs_scale=rhs[1][:],
+                out=acc,
+                lhsT=lhs[0][:, lhs_lo : lhs_lo + P].bitcast(lhs_fmt),
+                lhsT_scale=lhs[1][:, lhs_lo : lhs_lo + P],
+                rhs=rhs[0][:, rhs_lo:rhs_hi].bitcast(rhs_fmt),
+                rhs_scale=rhs[1][:, rhs_lo:rhs_hi],
                 start=start,
                 stop=stop,
             )
@@ -61,15 +58,20 @@ def tile_attend_gat_lse_k_kernel(tc, qT, kT, vT, doT, lse, delta, rw, qm, offs, 
         offsets = keep.tile([P, N // 16], U16, name="offsets")
         nc.sync.dma_start(offsets[:], offs)
 
-        def load_pool(name, pool, runs):
+        def load_planes(name, pool):
             planes = []
-            for lo, hi in runs:
-                piece = keep.tile([P, hi - lo, T], F32, name="%s_planes%d" % (name, lo))
-                nc.sync.dma_start(out=piece[:], in_=pool.rearrange("(p j) t -> p j t", j=PACK)[:, lo:hi, :])
-                planes.extend(piece[:, j, :] for j in range(hi - lo))
+            for j in range(PACK):
+                plane = sb("%s_plane%d" % (name, j), [P, T], F32)
+                nc.sync.dma_start(out=plane[:], in_=pool.rearrange("(p j) t -> p j t", j=PACK)[:, j, :])
+                planes.append(plane)
             return planes
 
-        k_planes = load_pool("k", kT, ((0, 2), (2, PACK)))
+        def load_columns(name, src, lo, hi, tag=None):
+            piece = sb(name, [P, PACK, hi - lo], F32, tag)
+            nc.sync.dma_start(out=piece[:], in_=src[0].rearrange("(p j) r -> p j r", j=PACK)[:, :, lo:hi])
+            return piece
+
+        k_planes = load_planes("k", kT)
         stat_rows = keep.tile([P, PASS], F32, name="stat_rows")
         nc.vector.memset(stat_rows[:], 0.0)
         for s, vec in enumerate((lse, delta, rw)):
@@ -77,17 +79,9 @@ def tile_attend_gat_lse_k_kernel(tc, qT, kT, vT, doT, lse, delta, rw, qm, offs, 
                 out=stat_rows[GROUPS * s : GROUPS * (s + 1), :],
                 in_=vec.rearrange("b (g c) o -> (b g) (c o)", g=GROUPS),
             )
-
-        q_raw = keep.tile([P, PACK, R], F32, name="q_raw", tag="query_raw")
-        nc.sync.dma_start(out=q_raw[:], in_=qT[0].rearrange("(p j) r -> p j r", j=PACK))
-
-        v_planes = load_pool("v", vT, ((0, 2), (2, 3), (3, PACK)))
-
-        do_raw = []
-        for lo, hi in DO_PIECES:
-            piece = keep.tile([P, PACK, hi - lo], F32, name="do_raw%d" % lo)
-            nc.sync.dma_start(out=piece[:], in_=doT[0].rearrange("(p j) r -> p j r", j=PACK)[:, :, lo:hi])
-            do_raw.append(piece)
+        q0_raw = load_columns("q0_raw", qT, 0, PASS)
+        v_planes = load_planes("v", vT)
+        do_raw = [load_columns("do_raw%d" % h, doT, h * HALF, (h + 1) * HALF) for h in range(2 * GROUPS)]
 
         windows = []
         for k in range(D // P):
@@ -109,178 +103,180 @@ def tile_attend_gat_lse_k_kernel(tc, qT, kT, vT, doT, lse, delta, rw, qm, offs, 
             out=neg_delta_rw[:], in0=stats[:, :, 2:4], scalar=-1.0, in1=stats[:, :, 4:6], op0=ALU.mult, op1=ALU.mult
         )
 
-        def interleave(engine_copy, grouped, planes, lo, hi, j0, j1):
-            engine_copy(
-                out=grouped[:, lo * PACK : hi * PACK].rearrange("p (c x j) -> p c j x", x=RUN, j=PACK)[:, :, j0:j1, :],
-                in_=planes[:, j0:j1, lo:hi].rearrange("p j (c x) -> p c j x", x=RUN),
+        def weave(copy, grouped, planes, j0, j1):
+            copy(
+                out=grouped.rearrange("p (c x j) -> p c j x", x=RUN, j=PACK)[:, :, j0:j1, :],
+                in_=planes[:, j0:j1, :].rearrange("p j (c x) -> p c j x", x=RUN),
             )
 
-        def gather_pool(name, planes, split):
-            picked = keep.tile([P, PACK, N], F32, name=name + "_picked", tag="picked")
-            grouped = grouped_tile(name + "_grouped")
-            for j in range(PACK):
-                nc.vector.tensor_copy(picked[:, j, :], planes[j].indirect(offsets[:]))
-                if split < N and j == 1:
-                    interleave(nc.vector.tensor_copy, grouped, picked, 0, N, 0, 2)
-            if split < N:
-                interleave(nc.vector.tensor_copy, grouped, picked, 0, split, 2, PACK)
-                interleave(nc.scalar.copy, grouped, picked, split, N, 2, PACK)
-            else:
-                interleave(nc.vector.tensor_copy, grouped, picked, 0, N, 0, PACK)
-            mx = mx_tiles(name, N)
-            quantize(mx, slice(0, N), grouped[:], E4M3)
-            return mx, picked
+        def deal(copy, pair, raw, m0, u):
+            width = raw.shape[2] // PACK
+            copy(
+                out=pair[:].rearrange("p (t m j) -> p m j t", t=2, j=PACK)[:, m0 : m0 + width, :, :],
+                in_=raw[:].rearrange("p j (m t) -> p m j t", t=PACK)[:, :, :, 2 * u : 2 * u + 2],
+            )
 
-        k_mx, k_picked = gather_pool("k", k_planes, N)
+        def pair_tiles(name, tag=None):
+            return [sb("%s_pair%d" % (name, u), [P, 2 * PASS], BF16, tag and "%s_pair%d" % (tag, u)) for u in range(2)]
+
+        def quantize_pair(mx, pairs, u, fmt):
+            quantize(mx, 2 * P * u, 2 * P * (u + 1), pairs[u][:], fmt)
+
+        k_picked = sb("k_picked", [P, PACK, N], F32)
+        for j in range(PACK):
+            vcopy(k_picked[:, j, :], k_planes[j][:].indirect(offsets[:]))
+        k_grouped = sb("k_grouped", [P, N * PACK], BF16)
+        weave(vcopy, k_grouped[:], k_picked, 0, PACK)
+        k_mx = mx_tiles("k", N)
+        quantize(k_mx, 0, N, k_grouped[:], E4M3)
+
+        q1_raw = [load_columns("q1_raw%d" % h, qT, PASS + h * HALF, PASS + (h + 1) * HALF, "k_plane%d" % h) for h in range(2)]
+        qm_rows = [qm[0, g * PASS : (g + 1) * PASS, :].rearrange("(p t) d -> p t d", t=PACK) for g in range(GROUPS)]
+        qm_first, qm_rest = [], []
+        for g in range(GROUPS):
+            qm_first.append(sb("qm_first%d" % g, [P, PACK, P], F32))
+            nc.sync.dma_start(out=qm_first[g][:], in_=qm_rows[g][:, :, 0:P])
+        for g in range(GROUPS):
+            qm_rest.append(sb("qm_rest%d" % g, [P, PACK, D - P], F32, "k_plane%d" % (2 + g)))
+            nc.sync.dma_start(out=qm_rest[g][:], in_=qm_rows[g][:, :, P:D])
+
         q_mx = [mx_tiles("q%d" % g, PASS) for g in range(GROUPS)]
-        for g in range(GROUPS):
-            grouped = grouped_tile("q_grouped%d" % g)
-            for t0 in (0, 2):
-                nc.vector.tensor_copy(
-                    out=grouped[:].rearrange("p (t m j) -> p m j t", t=PACK, j=PACK)[:, :, :, t0 : t0 + 2],
-                    in_=q_raw[:, :, g * PASS : (g + 1) * PASS].rearrange("p j (m t) -> p m j t", t=PACK)[:, :, :, t0 : t0 + 2],
-                )
-            quantize(q_mx[g], slice(0, PASS), grouped[:], E4M3)
+        q0_pairs = pair_tiles("q0")
+        for u in range(2):
+            deal(scopy, q0_pairs[u], q0_raw, 0, u)
+        for u in range(2):
+            quantize_pair(q_mx[0], q0_pairs, u, E4M3)
+        weights0 = sb("weights0", [P, PACK, N], F32)
+        for t in range(PACK):
+            acc = bank("score0", [P, N])
+            product(acc[:], q_mx[0], t * P, E4M3, k_mx, 0, N, E4M3)
+            nc.scalar.activation(out=weights0[:, t, :], in_=acc[:], func=ACT.Exp, bias=neg_lse[:, t, 0:1], scale=1.0)
 
-        qm_raw = keep.tile([P, GROUPS, PACK, D], F32, name="qm_raw", tag="query_raw")
-        for g in range(GROUPS):
-            nc.sync.dma_start(
-                out=qm_raw[:, g, :, :], in_=qm[0, g * PASS : (g + 1) * PASS, :].rearrange("(p t) d -> p t d", t=PACK)
-            )
-
-        weights = []
-        for g in range(GROUPS):
-            p_g = keep.tile([P, PACK, N], F32, name="weights%d" % g)
-            for t in range(PACK):
-                acc = bank("score", [P, N])
-                product(acc, q_mx[g], slice(t * P, (t + 1) * P), E4M3, k_mx, E4M3, True, True)
-                nc.scalar.activation(out=p_g[:, t, :], in_=acc[:], func=ACT.Exp, bias=neg_lse[:, t, g : g + 1], scale=1.0)
-            weights.append(p_g)
-
-        v_mx, v_picked = gather_pool("v", v_planes, V_SPLIT)
+        v_picked = [sb("v_picked%d" % h, [P, PACK, HALF], F32) for h in range(2)]
+        v_grouped = [sb("v_grouped%d" % h, [P, HALF * PACK], BF16) for h in range(2)]
+        v_mx = mx_tiles("v", N)
+        for j in range(PACK):
+            for h in range(2):
+                vcopy(v_picked[h][:, j, :], v_planes[j][:].indirect(offsets[:, h * HALF // 16 : (h + 1) * HALF // 16]))
+            if j == 1:
+                weave(scopy, v_grouped[0][:], v_picked[0], 0, 2)
+                weave(vcopy, v_grouped[1][:], v_picked[1], 0, 2)
+        weave(scopy, v_grouped[0][:], v_picked[0], 2, PACK)
+        weave(vcopy, v_grouped[1][:], v_picked[1], 2, PACK)
+        for h in (1, 0):
+            quantize(v_mx, h * HALF, (h + 1) * HALF, v_grouped[h][:], E4M3)
         warm = bank("warm", [P, N])
-        nc.tensor.transpose(warm[:, 0:P], v_picked[:, PACK - 1, 0:P], ident[:])
+        nc.tensor.transpose(warm[:, 0:P], v_picked[1][:, PACK - 1, 0:P], ident[:])
         for w in range(WARM_PASSES):
-            product(warm, q_mx[0], slice(0, P), E4M3, k_mx, E4M3, True, True)
+            product(warm[:], q_mx[0], 0, E4M3, k_mx, 0, N, E4M3)
 
         do_mx = [mx_tiles("do%d" % g, PASS) for g in range(GROUPS)]
         ds_mx = [mx_tiles("ds%d" % g, N) for g in range(GROUPS)]
-        do_grouped = [None] * GROUPS
 
-        def group_do(h, engine_copy, t0, t1):
-            lo, hi = DO_PIECES[h]
-            g = lo // PASS
-            if do_grouped[g] is None:
-                do_grouped[g] = grouped_tile("do_grouped%d" % g)
-            m0, m1 = (lo - g * PASS) // PACK, (hi - g * PASS) // PACK
-            engine_copy(
-                out=do_grouped[g][:].rearrange("p (t m j) -> p m j t", t=PACK, j=PACK)[:, m0:m1, :, t0:t1],
-                in_=do_raw[h][:].rearrange("p j (m t) -> p m j t", t=PACK)[:, :, :, t0:t1],
-            )
-
-        def grad_products(g, span):
-            accs = []
+        def centre(g, tag):
+            centred = sb("centred%d" % g, [P, PACK, N], F32, tag)
             for t in range(PACK):
-                cols = slice(t * P, (t + 1) * P)
-                if t % span == 0:
-                    quantize(
-                        do_mx[g], slice(t * P, (t + span) * P), do_grouped[g][:, t * PASS : (t + span) * PASS], E5M2
-                    )
                 acc = bank("dp", [P, N])
-                product(acc, do_mx[g], cols, E5M2, v_mx, E4M3, True, True)
-                accs.append(acc)
-            return accs
-
-        def ds_steps(g, accs):
-            steps = []
-            lo = 0
-            for width in DS_CHUNKS[g]:
-                centred = keep.tile([P, PACK, width], F32, name="centred%d_%d" % (g, lo))
-                grouped = keep.tile([P, width * PACK], BF16, name="ds_grouped%d_%d" % (g, lo), align_bytes=64)
-                steps.append((g, accs, centred, grouped, lo, lo + width))
-                lo += width
-            return steps
-
-        def centre(step):
-            g, accs, centred, grouped, lo, hi = step
-            for t in range(PACK):
+                product(acc[:], do_mx[g], t * P, E5M2, v_mx, 0, N, E4M3)
                 nc.scalar.activation(
-                    out=centred[:, t, :], in_=accs[t][:, lo:hi], func=ACT.Identity,
+                    out=centred[:, t, :], in_=acc[:], func=ACT.Identity,
                     bias=neg_delta_rw[:, t, g : g + 1], scale=stats[:, t, 4 + g : 5 + g],
                 )
+            return centred
 
-        def multiply(step):
-            g, accs, centred, grouped, lo, hi = step
+        do0_pairs = pair_tiles("do0")
+        deal(scopy, do0_pairs[0], do_raw[0], 0, 0)
+        deal(scopy, do0_pairs[1], do_raw[0], 0, 1)
+        deal(vcopy, do0_pairs[0], do_raw[1], HALF // PACK, 0)
+        deal(scopy, do0_pairs[1], do_raw[1], HALF // PACK, 1)
+        for u in range(2):
+            quantize_pair(do_mx[0], do0_pairs, u, E5M2)
+        centred0 = centre(0, None)
+
+        do1_pairs = pair_tiles("do1", "q0")
+        for h in range(2):
+            for u in range(2):
+                deal(vcopy, do1_pairs[u], do_raw[2 + h], h * HALF // PACK, u)
+        for u in range(2):
+            quantize_pair(do_mx[1], do1_pairs, u, E5M2)
+        centred1 = centre(1, "q0_raw")
+
+        q1_pairs = pair_tiles("q1")
+        for h in range(2):
+            for u in range(2):
+                deal(vcopy, q1_pairs[u], q1_raw[h], h * HALF // PACK, u)
+        for u in range(2):
+            quantize_pair(q_mx[1], q1_pairs, u, E4M3)
+        weights1 = []
+        for h in range(2):
+            weights1.append(sb("weights1_%d" % h, [P, PACK, HALF], F32, "v_plane%d" % h))
+            for u in range(2):
+                acc = bank("score1", [P, 2, HALF])
+                for e in range(2):
+                    product(acc[:, e, :], q_mx[1], (2 * u + e) * P, E4M3, k_mx, h * HALF, (h + 1) * HALF, E4M3)
+                for e in range(2):
+                    t = 2 * u + e
+                    nc.scalar.activation(
+                        out=weights1[h][:, t, :], in_=acc[:, e, :], func=ACT.Exp, bias=neg_lse[:, t, 1:2], scale=1.0
+                    )
+
+        ds_grouped = {}
+
+        def multiply(g, h):
+            cols = slice(h * HALF, (h + 1) * HALF)
+            weights = weights0[:, :, cols] if g == 0 else weights1[h][:]
+            centred = (centred0, centred1)[g][:, :, cols]
+            ds_grouped[g, h] = sb("ds_grouped%d_%d" % (g, h), [P, HALF * PACK], BF16)
             nc.vector.tensor_tensor(
-                out=grouped[:].rearrange("p (c x t) -> p c t x", x=2, t=PACK),
-                in0=weights[g][:, :, lo:hi].rearrange("p t (c x) -> p c t x", x=2),
-                in1=centred[:].rearrange("p t (c x) -> p c t x", x=2),
+                out=ds_grouped[g, h][:].rearrange("p (c x t) -> p c t x", x=2, t=PACK),
+                in0=weights.rearrange("p t (c x) -> p c t x", x=2),
+                in1=centred.rearrange("p t (c x) -> p c t x", x=2),
                 op=ALU.mult,
             )
 
-        def quantize_ds(step):
-            g, accs, centred, grouped, lo, hi = step
-            quantize(ds_mx[g], slice(lo, hi), grouped[:], E5M2)
+        def quantize_ds(g, h):
+            quantize(ds_mx[g], h * HALF, (h + 1) * HALF, ds_grouped[g, h][:], E5M2)
 
         qm_mx = [None] * (D // P)
         qm_grouped = [None] * (D // P)
 
-        def group_qm(k, engine_copy, tag):
-            qm_grouped[k] = keep.tile([P, GROUPS, P * PACK], BF16, name="qm_grouped%d" % k, tag=tag, align_bytes=64)
+        def weave_qm(k, copy, tag=None):
+            qm_grouped[k] = sb("qm_grouped%d" % k, [P, GROUPS, P * PACK], BF16, tag)
             for g in range(GROUPS):
-                engine_copy(
-                    out=qm_grouped[k][:, g, :].rearrange("p (c x t) -> p c t x", x=RUN, t=PACK),
-                    in_=qm_raw[:, g, :, k * P : (k + 1) * P].rearrange("p t (c x) -> p c t x", x=RUN),
-                )
+                rows = qm_first[g][:] if k == 0 else qm_rest[g][:, :, (k - 1) * P : k * P]
+                weave(copy, qm_grouped[k][:, g, :], rows, 0, PACK)
 
-        def quantize_qm(k, tag):
-            codes = keep.tile([P, GROUPS * P], U32, name="qm%d_codes" % k, tag=tag, align_bytes=64)
-            scales = keep.tile([P, GROUPS * P], U8, name="qm%d_scales" % k, align_bytes=64)
-            qm_mx[k] = (codes, scales)
-            quantize(qm_mx[k], slice(0, GROUPS * P), qm_grouped[k][:].rearrange("p g w -> p (g w)"), E4M3)
+        def quantize_qm(k, tag=None):
+            qm_mx[k] = mx_tiles("qm%d" % k, GROUPS * P, tag)
+            quantize(qm_mx[k], 0, GROUPS * P, qm_grouped[k][:].rearrange("p g w -> p (g w)"), E4M3)
 
-        group_do(0, nc.vector.tensor_copy, 0, 2)
-        group_do(0, nc.scalar.copy, 2, PACK)
-        group_do(1, nc.scalar.copy, 0, 2)
-        group_do(1, nc.scalar.copy, 2, PACK)
-        steps0 = ds_steps(0, grad_products(0, 2))
-        for step in steps0:
-            centre(step)
-        group_do(2, nc.vector.tensor_copy, 0, 2)
-        group_do(2, nc.vector.tensor_copy, 2, PACK)
-        steps1 = ds_steps(1, grad_products(1, 2))
-        for step in steps1:
-            centre(step)
-        group_qm(0, nc.scalar.copy, "qm_grouped0")
-        steps = steps0 + steps1
-        for s, step in enumerate(steps):
-            multiply(step)
-            if s == len(steps) - 1:
-                quantize_qm(0, "qm0_codes")
-            if s > 0:
-                quantize_ds(steps[s - 1])
-        quantize_ds(steps[-1])
+        weave_qm(0, scopy)
+        multiply(0, 0)
+        multiply(0, 1)
+        quantize_ds(0, 0)
+        multiply(1, 0)
+        quantize_ds(0, 1)
+        multiply(1, 1)
+        quantize_ds(1, 0)
+        quantize_qm(0)
+        quantize_ds(1, 1)
 
-        def finish(k, parts):
+        def finish(k):
             acc = bank("grad", [P, N])
             for g in range(GROUPS):
-                product(acc, qm_mx[k], slice(g * P, (g + 1) * P), E4M3, ds_mx[g], E5M2, g == 0, g == GROUPS - 1)
-            width = N // parts
-            for part in range(parts):
-                staged = keep.tile([P, width], F32, name="staged%d_%d" % (k, part), align_bytes=64)
-                nc.scalar.copy(out=staged[:], in_=acc[:, part * width : (part + 1) * width])
-                nc.vector.tensor_copy(
-                    windows[k][:].indirect(offsets[:, part * width // 16 : (part + 1) * width // 16]), staged[:]
-                )
+                product(acc[:], qm_mx[k], g * P, E4M3, ds_mx[g], 0, N, E5M2, g == 0, g == GROUPS - 1)
+            staged = sb("staged%d" % k, [P, N], F32)
+            nc.scalar.copy(out=staged[:], in_=acc[:])
+            vcopy(windows[k][:].indirect(offsets[:]), staged[:])
             nc.sync.dma_start(out=out[k * P : (k + 1) * P, :], in_=windows[k][:])
 
-        finish(0, 1)
-        group_qm(1, nc.scalar.copy, "qm_grouped1")
+        finish(0)
+        weave_qm(1, scopy)
         quantize_qm(1, "ds_grouped1_0")
-        finish(1, 1)
-        group_qm(2, nc.vector.tensor_copy, "ds_grouped1_256")
-        quantize_qm(2, "qm2_codes")
-        finish(2, 1)
-        group_qm(3, nc.scalar.copy, "qm_grouped3")
-        quantize_qm(3, "staged0_0")
-        finish(3, 1)
+        finish(1)
+        weave_qm(2, vcopy, "ds_grouped1_1")
+        quantize_qm(2)
+        finish(2)
+        weave_qm(3, scopy)
+        quantize_qm(3, "staged0")
+        finish(3)

@@ -55,23 +55,20 @@ def tile_attend_gat_lse_k_kernel(tc, qT, kT, vT, doT, lse, delta, rw, qm, offs, 
                 stop=stop,
             )
 
-        offsets = keep.tile([P, N // 16], U16, name="offsets")
-        nc.sync.dma_start(offsets[:], offs)
-
-        def load_planes(name, pool):
-            planes = []
-            for j in range(PACK):
-                plane = sb("%s_plane%d" % (name, j), [P, T], F32)
-                nc.sync.dma_start(out=plane[:], in_=pool.rearrange("(p j) t -> p j t", j=PACK)[:, j, :])
-                planes.append(plane)
-            return planes
+        def load_planes(name, pool, lo, hi):
+            piece = sb("%s_planes%d" % (name, lo), [P, hi - lo, T], F32)
+            nc.sync.dma_start(out=piece[:], in_=pool.rearrange("(p j) t -> p j t", j=PACK)[:, lo:hi, :])
+            return [piece[:, j, :] for j in range(hi - lo)]
 
         def load_columns(name, src, lo, hi, tag=None):
             piece = sb(name, [P, PACK, hi - lo], F32, tag)
             nc.sync.dma_start(out=piece[:], in_=src[0].rearrange("(p j) r -> p j r", j=PACK)[:, :, lo:hi])
             return piece
 
-        k_planes = load_planes("k", kT)
+        k_planes = load_planes("k", kT, 0, 2)
+        offsets = keep.tile([P, N // 16], U16, name="offsets")
+        nc.sync.dma_start(offsets[:], offs)
+        k_planes = k_planes + load_planes("k", kT, 2, PACK)
         stat_rows = keep.tile([P, PASS], F32, name="stat_rows")
         nc.vector.memset(stat_rows[:], 0.0)
         for s, vec in enumerate((lse, delta, rw)):
@@ -79,8 +76,8 @@ def tile_attend_gat_lse_k_kernel(tc, qT, kT, vT, doT, lse, delta, rw, qm, offs, 
                 out=stat_rows[GROUPS * s : GROUPS * (s + 1), :],
                 in_=vec.rearrange("b (g c) o -> (b g) (c o)", g=GROUPS),
             )
-        q0_raw = load_columns("q0_raw", qT, 0, PASS)
-        v_planes = load_planes("v", vT)
+        q_raw = load_columns("q_raw", qT, 0, R)
+        v_planes = load_planes("v", vT, 0, 2) + load_planes("v", vT, 2, 3) + load_planes("v", vT, 3, PACK)
         do_raw = [load_columns("do_raw%d" % h, doT, h * HALF, (h + 1) * HALF) for h in range(2 * GROUPS)]
 
         windows = []
@@ -113,7 +110,7 @@ def tile_attend_gat_lse_k_kernel(tc, qT, kT, vT, doT, lse, delta, rw, qm, offs, 
             width = raw.shape[2] // PACK
             copy(
                 out=pair[:].rearrange("p (t m j) -> p m j t", t=2, j=PACK)[:, m0 : m0 + width, :, :],
-                in_=raw[:].rearrange("p j (m t) -> p m j t", t=PACK)[:, :, :, 2 * u : 2 * u + 2],
+                in_=raw.rearrange("p j (m t) -> p m j t", t=PACK)[:, :, :, 2 * u : 2 * u + 2],
             )
 
         def pair_tiles(name, tag=None):
@@ -124,118 +121,110 @@ def tile_attend_gat_lse_k_kernel(tc, qT, kT, vT, doT, lse, delta, rw, qm, offs, 
 
         k_picked = sb("k_picked", [P, PACK, N], F32)
         for j in range(PACK):
-            vcopy(k_picked[:, j, :], k_planes[j][:].indirect(offsets[:]))
+            vcopy(k_picked[:, j, :], k_planes[j].indirect(offsets[:]))
         k_grouped = sb("k_grouped", [P, N * PACK], BF16)
         weave(vcopy, k_grouped[:], k_picked, 0, PACK)
         k_mx = mx_tiles("k", N)
         quantize(k_mx, 0, N, k_grouped[:], E4M3)
 
-        q1_raw = [load_columns("q1_raw%d" % h, qT, PASS + h * HALF, PASS + (h + 1) * HALF, "k_plane%d" % h) for h in range(2)]
         qm_rows = [qm[0, g * PASS : (g + 1) * PASS, :].rearrange("(p t) d -> p t d", t=PACK) for g in range(GROUPS)]
         qm_first, qm_rest = [], []
         for g in range(GROUPS):
             qm_first.append(sb("qm_first%d" % g, [P, PACK, P], F32))
             nc.sync.dma_start(out=qm_first[g][:], in_=qm_rows[g][:, :, 0:P])
         for g in range(GROUPS):
-            qm_rest.append(sb("qm_rest%d" % g, [P, PACK, D - P], F32, "k_plane%d" % (2 + g)))
+            qm_rest.append(sb("qm_rest%d" % g, [P, PACK, D - P], F32, "k_planes%d" % (2 * g)))
             nc.sync.dma_start(out=qm_rest[g][:], in_=qm_rows[g][:, :, P:D])
 
         q_mx = [mx_tiles("q%d" % g, PASS) for g in range(GROUPS)]
-        q0_pairs = pair_tiles("q0")
-        for u in range(2):
-            deal(scopy, q0_pairs[u], q0_raw, 0, u)
-        for u in range(2):
-            quantize_pair(q_mx[0], q0_pairs, u, E4M3)
-        weights0 = sb("weights0", [P, PACK, N], F32)
-        for t in range(PACK):
-            acc = bank("score0", [P, N])
-            product(acc[:], q_mx[0], t * P, E4M3, k_mx, 0, N, E4M3)
-            nc.scalar.activation(out=weights0[:, t, :], in_=acc[:], func=ACT.Exp, bias=neg_lse[:, t, 0:1], scale=1.0)
+        weights = []
+        for g in range(GROUPS):
+            pairs = pair_tiles("q%d" % g)
+            for u in range(2):
+                deal(vcopy, pairs[u], q_raw[:, :, g * PASS : (g + 1) * PASS], 0, u)
+            for u in range(2):
+                quantize_pair(q_mx[g], pairs, u, E4M3)
+            weights.append(sb("weights%d" % g, [P, PACK, N], F32))
+            for t in range(PACK):
+                acc = bank("score", [P, N])
+                product(acc[:], q_mx[g], t * P, E4M3, k_mx, 0, N, E4M3)
+                nc.scalar.activation(
+                    out=weights[g][:, t, :], in_=acc[:], func=ACT.Exp, bias=neg_lse[:, t, g : g + 1], scale=1.0
+                )
 
-        v_picked = [sb("v_picked%d" % h, [P, PACK, HALF], F32) for h in range(2)]
+        v_picked = sb("v_picked", [P, PACK - 1, N], F32, "k_picked")
         v_grouped = [sb("v_grouped%d" % h, [P, HALF * PACK], BF16) for h in range(2)]
         v_mx = mx_tiles("v", N)
-        for j in range(PACK):
-            for h in range(2):
-                vcopy(v_picked[h][:, j, :], v_planes[j][:].indirect(offsets[:, h * HALF // 16 : (h + 1) * HALF // 16]))
-            if j == 1:
-                weave(scopy, v_grouped[0][:], v_picked[0], 0, 2)
-                weave(vcopy, v_grouped[1][:], v_picked[1], 0, 2)
-        weave(scopy, v_grouped[0][:], v_picked[0], 2, PACK)
-        weave(vcopy, v_grouped[1][:], v_picked[1], 2, PACK)
-        for h in (1, 0):
+        for j in range(PACK - 1):
+            vcopy(v_picked[:, j, :], v_planes[j].indirect(offsets[:]))
+        for h in range(2):
+            weave(scopy, v_grouped[h][:], v_picked[:, :, h * HALF : (h + 1) * HALF], 0, 2)
+            vcopy(
+                out=v_grouped[h][:].rearrange("p (s j) -> p s j", j=PACK)[:, :, 2],
+                in_=v_picked[:, 2, h * HALF : (h + 1) * HALF],
+            )
+        for h in range(2):
+            vcopy(
+                v_grouped[h][:].rearrange("p (s j) -> p s j", j=PACK)[:, :, PACK - 1],
+                v_planes[PACK - 1].indirect(offsets[:, h * HALF // 16 : (h + 1) * HALF // 16]),
+            )
+        for h in range(2):
             quantize(v_mx, h * HALF, (h + 1) * HALF, v_grouped[h][:], E4M3)
         warm = bank("warm", [P, N])
-        nc.tensor.transpose(warm[:, 0:P], v_picked[1][:, PACK - 1, 0:P], ident[:])
         for w in range(WARM_PASSES):
-            product(warm[:], q_mx[0], 0, E4M3, k_mx, 0, N, E4M3)
+            product(warm[:], v_mx, 0, E4M3, k_mx, 0, N, E4M3)
 
         do_mx = [mx_tiles("do%d" % g, PASS) for g in range(GROUPS)]
         ds_mx = [mx_tiles("ds%d" % g, N) for g in range(GROUPS)]
 
-        def centre(g, tag):
-            centred = sb("centred%d" % g, [P, PACK, N], F32, tag)
+        def grad_products(g):
+            accs = []
             for t in range(PACK):
-                acc = bank("dp", [P, N])
-                product(acc[:], do_mx[g], t * P, E5M2, v_mx, 0, N, E4M3)
+                accs.append(bank("dp", [P, N]))
+                product(accs[t][:], do_mx[g], t * P, E5M2, v_mx, 0, N, E4M3)
+            return accs
+
+        def centre(g, accs, h):
+            centred = sb("centred%d_%d" % (g, h), [P, PACK, HALF], F32)
+            for t in range(PACK):
                 nc.scalar.activation(
-                    out=centred[:, t, :], in_=acc[:], func=ACT.Identity,
+                    out=centred[:, t, :], in_=accs[t][:, h * HALF : (h + 1) * HALF], func=ACT.Identity,
                     bias=neg_delta_rw[:, t, g : g + 1], scale=stats[:, t, 4 + g : 5 + g],
                 )
             return centred
 
-        do0_pairs = pair_tiles("do0")
-        deal(scopy, do0_pairs[0], do_raw[0], 0, 0)
-        deal(scopy, do0_pairs[1], do_raw[0], 0, 1)
-        deal(vcopy, do0_pairs[0], do_raw[1], HALF // PACK, 0)
-        deal(scopy, do0_pairs[1], do_raw[1], HALF // PACK, 1)
+        do_pairs = [pair_tiles("do%d" % g, "q%d" % g) for g in range(GROUPS)]
+        deal(scopy, do_pairs[0][0], do_raw[0][:], 0, 0)
+        deal(scopy, do_pairs[0][1], do_raw[0][:], 0, 1)
+        deal(vcopy, do_pairs[0][0], do_raw[1][:], HALF // PACK, 0)
+        deal(scopy, do_pairs[0][1], do_raw[1][:], HALF // PACK, 1)
         for u in range(2):
-            quantize_pair(do_mx[0], do0_pairs, u, E5M2)
-        centred0 = centre(0, None)
-
-        do1_pairs = pair_tiles("do1", "q0")
-        for h in range(2):
-            for u in range(2):
-                deal(vcopy, do1_pairs[u], do_raw[2 + h], h * HALF // PACK, u)
+            quantize_pair(do_mx[0], do_pairs[0], u, E5M2)
+        accs0 = grad_products(0)
+        centred = {(0, 0): centre(0, accs0, 0)}
+        deal(vcopy, do_pairs[1][0], do_raw[2][:], 0, 0)
+        deal(vcopy, do_pairs[1][1], do_raw[2][:], 0, 1)
+        deal(vcopy, do_pairs[1][0], do_raw[3][:], HALF // PACK, 0)
+        deal(vcopy, do_pairs[1][1], do_raw[3][:], HALF // PACK, 1)
+        centred[0, 1] = centre(0, accs0, 1)
         for u in range(2):
-            quantize_pair(do_mx[1], do1_pairs, u, E5M2)
-        centred1 = centre(1, "q0_raw")
-
-        q1_pairs = pair_tiles("q1")
-        for h in range(2):
-            for u in range(2):
-                deal(vcopy, q1_pairs[u], q1_raw[h], h * HALF // PACK, u)
-        for u in range(2):
-            quantize_pair(q_mx[1], q1_pairs, u, E4M3)
-        weights1 = []
-        for h in range(2):
-            weights1.append(sb("weights1_%d" % h, [P, PACK, HALF], F32, "v_plane%d" % h))
-            for u in range(2):
-                acc = bank("score1", [P, 2, HALF])
-                for e in range(2):
-                    product(acc[:, e, :], q_mx[1], (2 * u + e) * P, E4M3, k_mx, h * HALF, (h + 1) * HALF, E4M3)
-                for e in range(2):
-                    t = 2 * u + e
-                    nc.scalar.activation(
-                        out=weights1[h][:, t, :], in_=acc[:, e, :], func=ACT.Exp, bias=neg_lse[:, t, 1:2], scale=1.0
-                    )
+            quantize_pair(do_mx[1], do_pairs[1], u, E5M2)
+        accs1 = grad_products(1)
+        centred[1, 0] = centre(1, accs1, 0)
+        qm0_grouped = [sb("qm0_grouped%d" % g, [P, P * PACK], BF16) for g in range(GROUPS)]
+        weave(scopy, qm0_grouped[0][:], qm_first[0], 0, PACK)
+        centred[1, 1] = centre(1, accs1, 1)
 
         ds_grouped = {}
 
-        def multiply(g, h):
-            cols = slice(h * HALF, (h + 1) * HALF)
-            weights = weights0[:, :, cols] if g == 0 else weights1[h][:]
-            centred = (centred0, centred1)[g][:, :, cols]
-            ds_grouped[g, h] = sb("ds_grouped%d_%d" % (g, h), [P, HALF * PACK], BF16)
+        def multiply(name, weights, centred, tag=None):
+            ds_grouped[name] = sb(name, [P, weights.shape[2] * PACK], BF16, tag)
             nc.vector.tensor_tensor(
-                out=ds_grouped[g, h][:].rearrange("p (c x t) -> p c t x", x=2, t=PACK),
+                out=ds_grouped[name][:].rearrange("p (c x t) -> p c t x", x=2, t=PACK),
                 in0=weights.rearrange("p t (c x) -> p c t x", x=2),
                 in1=centred.rearrange("p t (c x) -> p c t x", x=2),
                 op=ALU.mult,
             )
-
-        def quantize_ds(g, h):
-            quantize(ds_mx[g], h * HALF, (h + 1) * HALF, ds_grouped[g, h][:], E5M2)
 
         qm_mx = [None] * (D // P)
         qm_grouped = [None] * (D // P)
@@ -243,23 +232,28 @@ def tile_attend_gat_lse_k_kernel(tc, qT, kT, vT, doT, lse, delta, rw, qm, offs, 
         def weave_qm(k, copy, tag=None):
             qm_grouped[k] = sb("qm_grouped%d" % k, [P, GROUPS, P * PACK], BF16, tag)
             for g in range(GROUPS):
-                rows = qm_first[g][:] if k == 0 else qm_rest[g][:, :, (k - 1) * P : k * P]
+                rows = qm_rest[g][:, :, (k - 1) * P : k * P]
                 weave(copy, qm_grouped[k][:, g, :], rows, 0, PACK)
 
         def quantize_qm(k, tag=None):
             qm_mx[k] = mx_tiles("qm%d" % k, GROUPS * P, tag)
             quantize(qm_mx[k], 0, GROUPS * P, qm_grouped[k][:].rearrange("p g w -> p (g w)"), E4M3)
 
-        weave_qm(0, scopy)
-        multiply(0, 0)
-        multiply(0, 1)
-        quantize_ds(0, 0)
-        multiply(1, 0)
-        quantize_ds(0, 1)
-        multiply(1, 1)
-        quantize_ds(1, 0)
-        quantize_qm(0)
-        quantize_ds(1, 1)
+        qm_mx[0] = mx_tiles("qm0", GROUPS * P)
+        weave(scopy, qm0_grouped[1][:], qm_first[1], 0, PACK)
+        steps = [(g, h) for g in range(GROUPS) for h in range(2)]
+
+        def quantize_ds(g, h):
+            quantize(ds_mx[g], h * HALF, (h + 1) * HALF, ds_grouped["ds_grouped%d_%d" % (g, h)][:], E5M2)
+
+        for i, (g, h) in enumerate(steps):
+            if i == len(steps) - 1:
+                quantize(qm_mx[0], 0, P, qm0_grouped[0][:], E4M3)
+            multiply("ds_grouped%d_%d" % (g, h), weights[g][:, :, h * HALF : (h + 1) * HALF], centred[g, h][:])
+            if i > 0:
+                quantize_ds(*steps[i - 1])
+        quantize(qm_mx[0], P, 2 * P, qm0_grouped[1][:], E4M3)
+        quantize_ds(*steps[-1])
 
         def finish(k):
             acc = bank("grad", [P, N])

@@ -152,22 +152,19 @@ def tile_attend_gat_lse_k_kernel(tc, qT, kT, vT, doT, lse, delta, rw, qm, offs, 
                     out=weights[g][:, t, :], in_=acc[:], func=ACT.Exp, bias=neg_lse[:, t, g : g + 1], scale=1.0
                 )
 
-        v_picked = sb("v_picked", [P, PACK - 1, N], F32, "k_picked")
+        v_picked = sb("v_picked", [P, 2, N], F32, "k_picked")
         v_grouped = [sb("v_grouped%d" % h, [P, HALF * PACK], BF16) for h in range(2)]
         v_mx = mx_tiles("v", N)
-        for j in range(PACK - 1):
+        for j in range(2):
             vcopy(v_picked[:, j, :], v_planes[j].indirect(offsets[:]))
         for h in range(2):
             weave(scopy, v_grouped[h][:], v_picked[:, :, h * HALF : (h + 1) * HALF], 0, 2)
-            vcopy(
-                out=v_grouped[h][:].rearrange("p (s j) -> p s j", j=PACK)[:, :, 2],
-                in_=v_picked[:, 2, h * HALF : (h + 1) * HALF],
-            )
-        for h in range(2):
-            vcopy(
-                v_grouped[h][:].rearrange("p (s j) -> p s j", j=PACK)[:, :, PACK - 1],
-                v_planes[PACK - 1].indirect(offsets[:, h * HALF // 16 : (h + 1) * HALF // 16]),
-            )
+        for j in range(2, PACK):
+            for h in range(2):
+                vcopy(
+                    v_grouped[h][:].rearrange("p (s j) -> p s j", j=PACK)[:, :, j],
+                    v_planes[j].indirect(offsets[:, h * HALF // 16 : (h + 1) * HALF // 16]),
+                )
         for h in range(2):
             quantize(v_mx, h * HALF, (h + 1) * HALF, v_grouped[h][:], E4M3)
         warm = bank("warm", [P, N])
@@ -193,22 +190,33 @@ def tile_attend_gat_lse_k_kernel(tc, qT, kT, vT, doT, lse, delta, rw, qm, offs, 
                 )
             return centred
 
-        do_pairs = [pair_tiles("do%d" % g, "q%d" % g) for g in range(GROUPS)]
+        do_pairs = [pair_tiles("do0", "q0")]
         deal(scopy, do_pairs[0][0], do_raw[0][:], 0, 0)
         deal(scopy, do_pairs[0][1], do_raw[0][:], 0, 1)
         deal(vcopy, do_pairs[0][0], do_raw[1][:], HALF // PACK, 0)
         deal(scopy, do_pairs[0][1], do_raw[1][:], HALF // PACK, 1)
         for u in range(2):
             quantize_pair(do_mx[0], do_pairs[0], u, E5M2)
+        do1_dealt = [[sb("do1_dealt%d_%d" % (h, u), [P, PASS], BF16, ("q1_pair%d" % u, None)[h]) for u in range(2)] for h in range(2)]
+
+        def deal_piece(copy, h, u):
+            deal(copy, do1_dealt[h][u], do_raw[2 + h][:], 0, u)
+
+        def quantize_piece(h, u):
+            for e in range(2):
+                lo = (2 * u + e) * P + h * P // 2
+                quantize(do_mx[1], lo, lo + P // 2, do1_dealt[h][u][:, e * HALF : (e + 1) * HALF], E5M2)
+
+        deal_piece(scopy, 0, 1)
         accs0 = grad_products(0)
-        centred = {(0, 0): centre(0, accs0, 0)}
-        deal(vcopy, do_pairs[1][0], do_raw[2][:], 0, 0)
-        deal(vcopy, do_pairs[1][1], do_raw[2][:], 0, 1)
-        deal(vcopy, do_pairs[1][0], do_raw[3][:], HALF // PACK, 0)
-        deal(vcopy, do_pairs[1][1], do_raw[3][:], HALF // PACK, 1)
-        centred[0, 1] = centre(0, accs0, 1)
+        centred = {(0, 0): centre(0, accs0, 0), (0, 1): centre(0, accs0, 1)}
+        deal_piece(vcopy, 0, 0)
+        quantize_piece(0, 0)
+        quantize_piece(0, 1)
         for u in range(2):
-            quantize_pair(do_mx[1], do_pairs[1], u, E5M2)
+            deal_piece(vcopy, 1, u)
+        for u in range(2):
+            quantize_piece(1, u)
         accs1 = grad_products(1)
         centred[1, 0] = centre(1, accs1, 0)
         qm0_grouped = [sb("qm0_grouped%d" % g, [P, P * PACK], BF16) for g in range(GROUPS)]
@@ -218,7 +226,7 @@ def tile_attend_gat_lse_k_kernel(tc, qT, kT, vT, doT, lse, delta, rw, qm, offs, 
         ds_grouped = {}
 
         def multiply(name, weights, centred, tag=None):
-            ds_grouped[name] = sb(name, [P, weights.shape[2] * PACK], BF16, tag)
+            ds_grouped[name] = sb(name, [P, weights.shape[2] * PACK], BF16, "k_grouped" if name == "ds_grouped0_0" else None)
             nc.vector.tensor_tensor(
                 out=ds_grouped[name][:].rearrange("p (c x t) -> p c t x", x=2, t=PACK),
                 in0=weights.rearrange("p t (c x) -> p c t x", x=2),
@@ -271,6 +279,6 @@ def tile_attend_gat_lse_k_kernel(tc, qT, kT, vT, doT, lse, delta, rw, qm, offs, 
         weave_qm(2, vcopy, "ds_grouped1_1")
         quantize_qm(2)
         finish(2)
-        weave_qm(3, scopy)
-        quantize_qm(3, "staged0")
+        weave_qm(3, scopy, "staged0")
+        quantize_qm(3, "staged1")
         finish(3)

@@ -171,8 +171,12 @@ def tile_attend_gat_lse_k_kernel(tc, qT, kT, vT, doT, lse, delta, rw, qm, offs, 
         for w in range(WARM_PASSES):
             product(warm[:], v_mx, 0, E4M3, k_mx, 0, N, E4M3)
 
-        do_mx = [mx_tiles("do%d" % g, PASS) for g in range(GROUPS)]
-        ds_mx = [mx_tiles("ds%d" % g, N) for g in range(GROUPS)]
+        grad_mx = mx_tiles("grad", PASS + GROUPS * N)
+        do_mx = [mx_tiles("do0", PASS), (grad_mx[0][:, 0:PASS], grad_mx[1][:, 0:PASS])]
+        ds_mx = [
+            (grad_mx[0][:, PASS + g * N : PASS + (g + 1) * N], grad_mx[1][:, PASS + g * N : PASS + (g + 1) * N])
+            for g in range(GROUPS)
+        ]
 
         def grad_products(g):
             accs = []
@@ -218,9 +222,8 @@ def tile_attend_gat_lse_k_kernel(tc, qT, kT, vT, doT, lse, delta, rw, qm, offs, 
         for u in range(2):
             quantize_piece(1, u)
         accs1 = grad_products(1)
-        centred[1, 0] = centre(1, accs1, 0)
         qm0_grouped = [sb("qm0_grouped%d" % g, [P, P * PACK], BF16) for g in range(GROUPS)]
-        weave(scopy, qm0_grouped[0][:], qm_first[0], 0, PACK)
+        centred[1, 0] = centre(1, accs1, 0)
         centred[1, 1] = centre(1, accs1, 1)
 
         ds_grouped = {}
@@ -249,19 +252,26 @@ def tile_attend_gat_lse_k_kernel(tc, qT, kT, vT, doT, lse, delta, rw, qm, offs, 
 
         qm_mx[0] = mx_tiles("qm0", GROUPS * P)
         weave(scopy, qm0_grouped[1][:], qm_first[1], 0, PACK)
-        steps = [(g, h) for g in range(GROUPS) for h in range(2)]
 
         def quantize_ds(g, h):
             quantize(ds_mx[g], h * HALF, (h + 1) * HALF, ds_grouped["ds_grouped%d_%d" % (g, h)][:], E5M2)
 
-        for i, (g, h) in enumerate(steps):
-            if i == len(steps) - 1:
-                quantize(qm_mx[0], 0, P, qm0_grouped[0][:], E4M3)
+        def multiply_ds(g, h):
             multiply("ds_grouped%d_%d" % (g, h), weights[g][:, :, h * HALF : (h + 1) * HALF], centred[g, h][:])
-            if i > 0:
-                quantize_ds(*steps[i - 1])
+
+        multiply_ds(0, 0)
+        multiply_ds(0, 1)
+        weave(vcopy, qm0_grouped[0][:], qm_first[0], 0, PACK)
+        quantize_ds(0, 0)
+        quantize(qm_mx[0], 0, P, qm0_grouped[0][:], E4M3)
+        multiply_ds(1, 0)
+        quantize_ds(0, 1)
+        quantize_ds(1, 0)
         quantize(qm_mx[0], P, 2 * P, qm0_grouped[1][:], E4M3)
-        quantize_ds(*steps[-1])
+        multiply_ds(1, 1)
+        weave_qm(1, scopy)
+        quantize_qm(1, "ds_grouped1_0")
+        quantize_ds(1, 1)
 
         def finish(k):
             acc = bank("grad", [P, N])
@@ -272,13 +282,24 @@ def tile_attend_gat_lse_k_kernel(tc, qT, kT, vT, doT, lse, delta, rw, qm, offs, 
             vcopy(windows[k][:].indirect(offsets[:]), staged[:])
             nc.sync.dma_start(out=out[k * P : (k + 1) * P, :], in_=windows[k][:])
 
-        finish(0)
-        weave_qm(1, scopy)
-        quantize_qm(1, "ds_grouped1_0")
+        early = bank("early", [P, N])
+        late = bank("late", [P, N])
+        for g in range(GROUPS):
+            lo = PASS + g * N - HALF
+            product(early[:], qm_mx[0], g * P, E4M3, grad_mx, lo, lo + N, E5M2, g == 0, g == GROUPS - 1)
+            if g == 0:
+                warm = bank("warm", [P, N])
+                product(warm[:], qm_mx[0], 0, E4M3, grad_mx, lo, lo + N, E5M2)
+            product(late[:], qm_mx[0], g * P, E4M3, ds_mx[g], 0, N, E5M2, g == 0, g == GROUPS - 1)
+        for h, acc in enumerate((early, late)):
+            staged = sb("staged0_%d" % h, [P, HALF], F32, ("staged0_0", "staged0")[h])
+            nc.scalar.copy(out=staged[:], in_=acc[:, HALF:N])
+            vcopy(windows[0][:].indirect(offsets[:, h * HALF // 16 : (h + 1) * HALF // 16]), staged[:])
+        nc.sync.dma_start(out=out[0:P, :], in_=windows[0][:])
         finish(1)
-        weave_qm(2, vcopy, "ds_grouped1_1")
+        weave_qm(2, scopy, "staged0")
         quantize_qm(2)
+        weave_qm(3, scopy, "staged1")
         finish(2)
-        weave_qm(3, scopy, "staged0")
-        quantize_qm(3, "staged1")
+        quantize_qm(3)
         finish(3)

@@ -273,11 +273,11 @@ def tile_attend_gat_lse_k_kernel(tc, qT, kT, vT, doT, lse, delta, rw, qm, offs, 
         quantize_qm(1, "ds_grouped1_0")
         quantize_ds(1, 1)
 
-        def finish(k):
+        def finish(k, tag=None):
             acc = bank("grad", [P, N])
             for g in range(GROUPS):
                 product(acc[:], qm_mx[k], g * P, E4M3, ds_mx[g], 0, N, E5M2, g == 0, g == GROUPS - 1)
-            staged = sb("staged%d" % k, [P, N], F32)
+            staged = sb("staged%d" % k, [P, N], F32, tag)
             nc.scalar.copy(out=staged[:], in_=acc[:])
             vcopy(windows[k][:].indirect(offsets[:]), staged[:])
             nc.sync.dma_start(out=out[k * P : (k + 1) * P, :], in_=windows[k][:])
@@ -295,11 +295,12 @@ def tile_attend_gat_lse_k_kernel(tc, qT, kT, vT, doT, lse, delta, rw, qm, offs, 
             staged = sb("staged0_%d" % h, [P, HALF], F32, ("staged0_0", "staged0")[h])
             nc.scalar.copy(out=staged[:], in_=acc[:, HALF:N])
             vcopy(windows[0][:].indirect(offsets[:, h * HALF // 16 : (h + 1) * HALF // 16]), staged[:])
+            if h == 0:
+                weave_qm(2, scopy, "ds_grouped0_1")
+                quantize_qm(2)
         nc.sync.dma_start(out=out[0:P, :], in_=windows[0][:])
         finish(1)
-        weave_qm(2, scopy, "staged0")
-        quantize_qm(2)
-        weave_qm(3, scopy, "staged1")
-        finish(2)
+        weave_qm(3, scopy, "staged0")
         quantize_qm(3)
+        finish(2, "staged0")
         finish(3)

@@ -240,11 +240,11 @@ def tile_attend_gat_lse_k_kernel(tc, qT, kT, vT, doT, lse, delta, rw, qm, offs, 
         qm_mx = [None] * (D // P)
         qm_grouped = [None] * (D // P)
 
-        def weave_qm(k, copy, tag=None):
+        def weave_qm(k, copies, tag=None):
             qm_grouped[k] = sb("qm_grouped%d" % k, [P, GROUPS, P * PACK], BF16, tag)
             for g in range(GROUPS):
                 rows = qm_rest[g][:, :, (k - 1) * P : k * P]
-                weave(copy, qm_grouped[k][:, g, :], rows, 0, PACK)
+                weave(copies[g], qm_grouped[k][:, g, :], rows, 0, PACK)
 
         def quantize_qm(k, tag=None):
             qm_mx[k] = mx_tiles("qm%d" % k, GROUPS * P, tag)
@@ -269,7 +269,7 @@ def tile_attend_gat_lse_k_kernel(tc, qT, kT, vT, doT, lse, delta, rw, qm, offs, 
         quantize_ds(1, 0)
         quantize(qm_mx[0], P, 2 * P, qm0_grouped[1][:], E4M3)
         multiply_ds(1, 1)
-        weave_qm(1, scopy)
+        weave_qm(1, (scopy, scopy))
         quantize_qm(1, "ds_grouped1_0")
         quantize_ds(1, 1)
 
@@ -287,20 +287,17 @@ def tile_attend_gat_lse_k_kernel(tc, qT, kT, vT, doT, lse, delta, rw, qm, offs, 
         for g in range(GROUPS):
             lo = PASS + g * N - HALF
             product(early[:], qm_mx[0], g * P, E4M3, grad_mx, lo, lo + N, E5M2, g == 0, g == GROUPS - 1)
-            if g == 0:
-                warm = bank("warm", [P, N])
-                product(warm[:], qm_mx[0], 0, E4M3, grad_mx, lo, lo + N, E5M2)
             product(late[:], qm_mx[0], g * P, E4M3, ds_mx[g], 0, N, E5M2, g == 0, g == GROUPS - 1)
         for h, acc in enumerate((early, late)):
             staged = sb("staged0_%d" % h, [P, HALF], F32, ("staged0_0", "staged0")[h])
             nc.scalar.copy(out=staged[:], in_=acc[:, HALF:N])
             vcopy(windows[0][:].indirect(offsets[:, h * HALF // 16 : (h + 1) * HALF // 16]), staged[:])
             if h == 0:
-                weave_qm(2, scopy, "ds_grouped0_1")
-                quantize_qm(2)
+                weave_qm(2, (scopy, vcopy), "ds_grouped0_1")
         nc.sync.dma_start(out=out[0:P, :], in_=windows[0][:])
+        quantize_qm(2, "staged0")
         finish(1)
-        weave_qm(3, scopy, "staged0")
+        weave_qm(3, (scopy, scopy), "ds_grouped0_1")
         quantize_qm(3)
-        finish(2, "staged0")
+        finish(2)
         finish(3)

@@ -73,7 +73,7 @@ def tile_attend_gat_lse_k_kernel(tc, qT, kT, vT, doT, lse, delta, rw, qm, offs, 
         nc.vector.memset(stat_rows[:], 0.0)
         for s, vec in enumerate((lse, delta, rw)):
             nc.sync.dma_start(
-                out=stat_rows[GROUPS * s : GROUPS * (s + 1), :],
+                out=stat_rows[4 * s : P : P // GROUPS, :],
                 in_=vec.rearrange("b (g c) o -> (b g) (c o)", g=GROUPS),
             )
         q_raw = load_columns("q_raw", qT, 0, R)
@@ -91,13 +91,13 @@ def tile_attend_gat_lse_k_kernel(tc, qT, kT, vT, doT, lse, delta, rw, qm, offs, 
         stat_bank = bank("stat_bank", [P, PACK, P])
         for t in range(PACK):
             nc.tensor.transpose(stat_bank[:, t, :], stat_rows[:, t:PASS:PACK], ident[:])
-        stats = keep.tile([P, PACK, 8], F32, name="stats")
-        nc.vector.tensor_copy(out=stats[:], in_=stat_bank[:, :, 0:8])
+        stats = keep.tile([P, PACK, GROUPS, 3], F32, name="stats")
+        nc.vector.tensor_copy(out=stats[:], in_=stat_bank[:].rearrange("p t (g x) -> p t g x", g=GROUPS)[:, :, :, 0:12:4])
         neg_lse = keep.tile([P, PACK, GROUPS], F32, name="neg_lse")
-        nc.vector.tensor_scalar(out=neg_lse[:], in0=stats[:, :, 0:2], scalar1=-1.0, scalar2=None, op0=ALU.mult)
+        nc.vector.tensor_scalar(out=neg_lse[:], in0=stats[:, :, :, 0], scalar1=-1.0, scalar2=None, op0=ALU.mult)
         neg_delta_rw = keep.tile([P, PACK, GROUPS], F32, name="neg_delta_rw")
         nc.vector.scalar_tensor_tensor(
-            out=neg_delta_rw[:], in0=stats[:, :, 2:4], scalar=-1.0, in1=stats[:, :, 4:6], op0=ALU.mult, op1=ALU.mult
+            out=neg_delta_rw[:], in0=stats[:, :, :, 1], scalar=-1.0, in1=stats[:, :, :, 2], op0=ALU.mult, op1=ALU.mult
         )
 
         def weave(copy, grouped, planes, j0, j1):
@@ -190,7 +190,7 @@ def tile_attend_gat_lse_k_kernel(tc, qT, kT, vT, doT, lse, delta, rw, qm, offs, 
             for t in range(PACK):
                 nc.scalar.activation(
                     out=centred[:, t, :], in_=accs[t][:, h * HALF : (h + 1) * HALF], func=ACT.Identity,
-                    bias=neg_delta_rw[:, t, g : g + 1], scale=stats[:, t, 4 + g : 5 + g],
+                    bias=neg_delta_rw[:, t, g : g + 1], scale=stats[:, t, g, 2:3],
                 )
             return centred
 

@@ -186,7 +186,7 @@ def tile_attend_gat_lse_k_kernel(tc, qT, kT, vT, doT, lse, delta, rw, qm, offs, 
             return accs
 
         def centre(g, accs, h):
-            centred = sb("centred%d_%d" % (g, h), [P, PACK, HALF], F32)
+            centred = sb("centred%d_%d" % (g, h), [P, PACK, HALF], F32, "q1_pair1" if (g, h) == (0, 1) else None)
             for t in range(PACK):
                 nc.scalar.activation(
                     out=centred[:, t, :], in_=accs[t][:, h * HALF : (h + 1) * HALF], func=ACT.Identity,
@@ -194,33 +194,36 @@ def tile_attend_gat_lse_k_kernel(tc, qT, kT, vT, doT, lse, delta, rw, qm, offs, 
                 )
             return centred
 
-        do_pairs = [pair_tiles("do0", "q0")]
-        deal(scopy, do_pairs[0][0], do_raw[0][:], 0, 0)
-        deal(scopy, do_pairs[0][1], do_raw[0][:], 0, 1)
-        deal(vcopy, do_pairs[0][0], do_raw[1][:], HALF // PACK, 0)
-        deal(scopy, do_pairs[0][1], do_raw[1][:], HALF // PACK, 1)
-        for u in range(2):
-            quantize_pair(do_mx[0], do_pairs[0], u, E5M2)
-        do1_dealt = [[sb("do1_dealt%d_%d" % (h, u), [P, PASS], BF16, ("q1_pair%d" % u, None)[h]) for u in range(2)] for h in range(2)]
+        dealt_tags = (("q0_pair0", "q0_pair1"), (None, None), ("q1_pair0", "q1_pair1"), (None, None))
+        dealt = [[sb("do_dealt%d_%d" % (i, u), [P, PASS], BF16, dealt_tags[i][u]) for u in range(2)] for i in range(2 * GROUPS)]
 
-        def deal_piece(copy, h, u):
-            deal(copy, do1_dealt[h][u], do_raw[2 + h][:], 0, u)
+        def deal_piece(copy, i, u):
+            deal(copy, dealt[i][u], do_raw[i][:], 0, u)
 
-        def quantize_piece(h, u):
+        def quantize_piece(i, u):
             for e in range(2):
-                lo = (2 * u + e) * P + h * P // 2
-                quantize(do_mx[1], lo, lo + P // 2, do1_dealt[h][u][:, e * HALF : (e + 1) * HALF], E5M2)
+                lo = (2 * u + e) * P + (i % 2) * P // 2
+                quantize(do_mx[i // 2], lo, lo + P // 2, dealt[i][u][:, e * HALF : (e + 1) * HALF], E5M2)
 
+        deal_piece(scopy, 0, 0)
         deal_piece(scopy, 0, 1)
-        accs0 = grad_products(0)
-        centred = {(0, 0): centre(0, accs0, 0), (0, 1): centre(0, accs0, 1)}
-        deal_piece(vcopy, 0, 0)
         quantize_piece(0, 0)
+        deal_piece(vcopy, 1, 0)
+        deal_piece(scopy, 1, 1)
         quantize_piece(0, 1)
+        quantize_piece(1, 0)
+        quantize_piece(1, 1)
+        accs0 = grad_products(0)
+        centred = {(0, 0): centre(0, accs0, 0)}
         for u in range(2):
-            deal_piece(vcopy, 1, u)
+            deal_piece(vcopy, 2, u)
+        quantize_piece(2, 0)
+        quantize_piece(2, 1)
+        centred[0, 1] = centre(0, accs0, 1)
         for u in range(2):
-            quantize_piece(1, u)
+            deal_piece(vcopy, 3, u)
+        for u in range(2):
+            quantize_piece(3, u)
         accs1 = grad_products(1)
         qm0_grouped = [sb("qm0_grouped%d" % g, [P, P * PACK], BF16) for g in range(GROUPS)]
         centred[1, 0] = centre(1, accs1, 0)
@@ -259,9 +262,9 @@ def tile_attend_gat_lse_k_kernel(tc, qT, kT, vT, doT, lse, delta, rw, qm, offs, 
         def multiply_ds(g, h):
             multiply("ds_grouped%d_%d" % (g, h), weights[g][:, :, h * HALF : (h + 1) * HALF], centred[g, h][:])
 
+        weave(vcopy, qm0_grouped[0][:], qm_first[0], 0, PACK)
         multiply_ds(0, 0)
         multiply_ds(0, 1)
-        weave(vcopy, qm0_grouped[0][:], qm_first[0], 0, PACK)
         quantize_ds(0, 0)
         quantize(qm_mx[0], 0, P, qm0_grouped[0][:], E4M3)
         multiply_ds(1, 0)
@@ -275,8 +278,8 @@ def tile_attend_gat_lse_k_kernel(tc, qT, kT, vT, doT, lse, delta, rw, qm, offs, 
 
         def finish(k, tag=None):
             acc = bank("grad", [P, N])
-            for g in range(GROUPS):
-                product(acc[:], qm_mx[k], g * P, E4M3, ds_mx[g], 0, N, E5M2, g == 0, g == GROUPS - 1)
+            for g in reversed(range(GROUPS)):
+                product(acc[:], qm_mx[k], g * P, E4M3, ds_mx[g], 0, N, E5M2, g == GROUPS - 1, g == 0)
             staged = sb("staged%d" % k, [P, N], F32, tag)
             nc.scalar.copy(out=staged[:], in_=acc[:])
             vcopy(windows[k][:].indirect(offsets[:]), staged[:])

@@ -65,10 +65,10 @@ def tile_attend_gat_lse_k_kernel(tc, qT, kT, vT, doT, lse, delta, rw, qm, offs, 
             nc.sync.dma_start(out=piece[:], in_=src[0].rearrange("(p j) r -> p j r", j=PACK)[:, :, lo:hi])
             return piece
 
-        k_planes = load_planes("k", kT, 0, 2)
+        v_planes = load_planes("v", vT, 0, 2)
         offsets = keep.tile([P, N // 16], U16, name="offsets")
         nc.sync.dma_start(offsets[:], offs)
-        k_planes = k_planes + load_planes("k", kT, 2, PACK)
+        v_planes = v_planes + load_planes("v", vT, 2, PACK)
         stat_rows = keep.tile([P, PASS], F32, name="stat_rows")
         nc.vector.memset(stat_rows[:], 0.0)
         for s, vec in enumerate((lse, delta, rw)):
@@ -76,9 +76,9 @@ def tile_attend_gat_lse_k_kernel(tc, qT, kT, vT, doT, lse, delta, rw, qm, offs, 
                 out=stat_rows[4 * s : P : P // GROUPS, :],
                 in_=vec.rearrange("b (g c) o -> (b g) (c o)", g=GROUPS),
             )
-        q_raw = load_columns("q_raw", qT, 0, R)
-        v_planes = load_planes("v", vT, 0, 2) + load_planes("v", vT, 2, 3) + load_planes("v", vT, 3, PACK)
-        do_raw = [load_columns("do_raw%d" % h, doT, h * HALF, (h + 1) * HALF) for h in range(2 * GROUPS)]
+        do_raw = load_columns("do_raw", doT, 0, R)
+        k_planes = load_planes("k", kT, 0, 2) + load_planes("k", kT, 2, 3) + load_planes("k", kT, 3, PACK)
+        q_raw = [load_columns("q_raw%d" % h, qT, h * HALF, (h + 1) * HALF) for h in range(2 * GROUPS)]
 
         windows = []
         for k in range(D // P):
@@ -119,13 +119,13 @@ def tile_attend_gat_lse_k_kernel(tc, qT, kT, vT, doT, lse, delta, rw, qm, offs, 
         def quantize_pair(mx, pairs, u, fmt):
             quantize(mx, 2 * P * u, 2 * P * (u + 1), pairs[u][:], fmt)
 
-        k_picked = sb("k_picked", [P, PACK, N], F32)
+        v_picked = sb("v_picked", [P, PACK, N], F32)
         for j in range(PACK):
-            vcopy(k_picked[:, j, :], k_planes[j].indirect(offsets[:]))
-        k_grouped = sb("k_grouped", [P, N * PACK], BF16)
-        weave(vcopy, k_grouped[:], k_picked, 0, PACK)
-        k_mx = mx_tiles("k", N)
-        quantize(k_mx, 0, N, k_grouped[:], E4M3)
+            vcopy(v_picked[:, j, :], v_planes[j].indirect(offsets[:]))
+        v_grouped = sb("v_grouped", [P, N * PACK], BF16)
+        weave(vcopy, v_grouped[:], v_picked, 0, PACK)
+        v_mx = mx_tiles("v", N)
+        quantize(v_mx, 0, N, v_grouped[:], E4M3)
 
         qm_rows = [qm[0, g * PASS : (g + 1) * PASS, :].rearrange("(p t) d -> p t d", t=PACK) for g in range(GROUPS)]
         qm_first, qm_rest = [], []
@@ -133,43 +133,8 @@ def tile_attend_gat_lse_k_kernel(tc, qT, kT, vT, doT, lse, delta, rw, qm, offs, 
             qm_first.append(sb("qm_first%d" % g, [P, PACK, P], F32))
             nc.sync.dma_start(out=qm_first[g][:], in_=qm_rows[g][:, :, 0:P])
         for g in range(GROUPS):
-            qm_rest.append(sb("qm_rest%d" % g, [P, PACK, D - P], F32, "k_planes%d" % (2 * g)))
+            qm_rest.append(sb("qm_rest%d" % g, [P, PACK, D - P], F32, "v_planes%d" % (2 * g)))
             nc.sync.dma_start(out=qm_rest[g][:], in_=qm_rows[g][:, :, P:D])
-
-        q_mx = [mx_tiles("q%d" % g, PASS) for g in range(GROUPS)]
-        weights = []
-        for g in range(GROUPS):
-            pairs = pair_tiles("q%d" % g)
-            for u in range(2):
-                deal(vcopy, pairs[u], q_raw[:, :, g * PASS : (g + 1) * PASS], 0, u)
-            for u in range(2):
-                quantize_pair(q_mx[g], pairs, u, E4M3)
-            weights.append(sb("weights%d" % g, [P, PACK, N], F32))
-            for t in range(PACK):
-                acc = bank("score", [P, N])
-                product(acc[:], q_mx[g], t * P, E4M3, k_mx, 0, N, E4M3)
-                nc.scalar.activation(
-                    out=weights[g][:, t, :], in_=acc[:], func=ACT.Exp, bias=neg_lse[:, t, g : g + 1], scale=1.0
-                )
-
-        v_picked = sb("v_picked", [P, 2, N], F32, "k_picked")
-        v_grouped = [sb("v_grouped%d" % h, [P, HALF * PACK], BF16) for h in range(2)]
-        v_mx = mx_tiles("v", N)
-        for j in range(2):
-            vcopy(v_picked[:, j, :], v_planes[j].indirect(offsets[:]))
-        for h in range(2):
-            weave(scopy, v_grouped[h][:], v_picked[:, :, h * HALF : (h + 1) * HALF], 0, 2)
-        for j in range(2, PACK):
-            for h in range(2):
-                vcopy(
-                    v_grouped[h][:].rearrange("p (s j) -> p s j", j=PACK)[:, :, j],
-                    v_planes[j].indirect(offsets[:, h * HALF // 16 : (h + 1) * HALF // 16]),
-                )
-        for h in range(2):
-            quantize(v_mx, h * HALF, (h + 1) * HALF, v_grouped[h][:], E4M3)
-        warm = bank("warm", [P, N])
-        for w in range(WARM_PASSES):
-            product(warm[:], v_mx, 0, E4M3, k_mx, 0, N, E4M3)
 
         grad_mx = mx_tiles("grad", PASS + GROUPS * N)
         do_mx = [mx_tiles("do0", PASS), (grad_mx[0][:, 0:PASS], grad_mx[1][:, 0:PASS])]
@@ -177,33 +142,72 @@ def tile_attend_gat_lse_k_kernel(tc, qT, kT, vT, doT, lse, delta, rw, qm, offs, 
             (grad_mx[0][:, PASS + g * N : PASS + (g + 1) * N], grad_mx[1][:, PASS + g * N : PASS + (g + 1) * N])
             for g in range(GROUPS)
         ]
-
-        def grad_products(g):
-            accs = []
+        centred = []
+        for g in range(GROUPS):
+            pairs = pair_tiles("do%d" % g)
+            for u in range(2):
+                deal(vcopy, pairs[u], do_raw[:, :, g * PASS : (g + 1) * PASS], 0, u)
+            for u in range(2):
+                quantize_pair(do_mx[g], pairs, u, E5M2)
+            centred.append(sb("centred%d" % g, [P, PACK, N], F32))
             for t in range(PACK):
-                accs.append(bank("dp", [P, N]))
-                product(accs[t][:], do_mx[g], t * P, E5M2, v_mx, 0, N, E4M3)
-            return accs
-
-        def centre(g, accs, h):
-            centred = sb("centred%d_%d" % (g, h), [P, PACK, HALF], F32, "q1_pair1" if (g, h) == (0, 1) else None)
-            for t in range(PACK):
+                acc = bank("dp", [P, N])
+                product(acc[:], do_mx[g], t * P, E5M2, v_mx, 0, N, E4M3)
                 nc.scalar.activation(
-                    out=centred[:, t, :], in_=accs[t][:, h * HALF : (h + 1) * HALF], func=ACT.Identity,
+                    out=centred[g][:, t, :], in_=acc[:], func=ACT.Identity,
                     bias=neg_delta_rw[:, t, g : g + 1], scale=stats[:, t, g, 2:3],
                 )
-            return centred
 
-        dealt_tags = (("q0_pair0", "q0_pair1"), (None, None), ("q1_pair0", "q1_pair1"), (None, None))
-        dealt = [[sb("do_dealt%d_%d" % (i, u), [P, PASS], BF16, dealt_tags[i][u]) for u in range(2)] for i in range(2 * GROUPS)]
+        k_picked = sb("k_picked", [P, 2, N], F32, "v_picked")
+        k_grouped = [sb("k_grouped%d" % h, [P, HALF * PACK], BF16) for h in range(2)]
+        k_mx = mx_tiles("k", N)
+        for j in range(2):
+            vcopy(k_picked[:, j, :], k_planes[j].indirect(offsets[:]))
+        for h in range(2):
+            weave(scopy, k_grouped[h][:], k_picked[:, :, h * HALF : (h + 1) * HALF], 0, 2)
+        for j in range(2, PACK):
+            for h in range(2):
+                vcopy(
+                    k_grouped[h][:].rearrange("p (s j) -> p s j", j=PACK)[:, :, j],
+                    k_planes[j].indirect(offsets[:, h * HALF // 16 : (h + 1) * HALF // 16]),
+                )
+        for h in range(2):
+            quantize(k_mx, h * HALF, (h + 1) * HALF, k_grouped[h][:], E4M3)
+        warm = bank("warm", [P, N])
+        for w in range(WARM_PASSES):
+            product(warm[:], k_mx, 0, E4M3, v_mx, 0, N, E4M3)
+
+        q_mx = [mx_tiles("q%d" % g, PASS) for g in range(GROUPS)]
+
+        def score_products(g):
+            accs = []
+            for h in range(2):
+                for u in range(2):
+                    accs.append(bank("score", [P, 2, HALF]))
+                    for e in range(2):
+                        lhs_lo = (2 * u + e) * P
+                        product(accs[-1][:, e, :], q_mx[g], lhs_lo, E4M3, k_mx, h * HALF, (h + 1) * HALF, E4M3)
+            return accs
+
+        def weigh(g, accs, h):
+            weights = sb("weights%d_%d" % (g, h), [P, PACK, HALF], F32, "do1_pair1" if (g, h) == (0, 1) else None)
+            for t in range(PACK):
+                nc.scalar.activation(
+                    out=weights[:, t, :], in_=accs[2 * h + t // 2][:, t % 2, :], func=ACT.Exp,
+                    bias=neg_lse[:, t, g : g + 1], scale=1.0,
+                )
+            return weights
+
+        dealt_tags = (("do0_pair0", "do0_pair1"), (None, None), ("do1_pair0", "do1_pair1"), (None, None))
+        dealt = [[sb("q_dealt%d_%d" % (i, u), [P, PASS], BF16, dealt_tags[i][u]) for u in range(2)] for i in range(2 * GROUPS)]
 
         def deal_piece(copy, i, u):
-            deal(copy, dealt[i][u], do_raw[i][:], 0, u)
+            deal(copy, dealt[i][u], q_raw[i][:], 0, u)
 
         def quantize_piece(i, u):
             for e in range(2):
                 lo = (2 * u + e) * P + (i % 2) * P // 2
-                quantize(do_mx[i // 2], lo, lo + P // 2, dealt[i][u][:, e * HALF : (e + 1) * HALF], E5M2)
+                quantize(q_mx[i // 2], lo, lo + P // 2, dealt[i][u][:, e * HALF : (e + 1) * HALF], E4M3)
 
         deal_piece(scopy, 0, 0)
         deal_piece(scopy, 0, 1)
@@ -213,26 +217,26 @@ def tile_attend_gat_lse_k_kernel(tc, qT, kT, vT, doT, lse, delta, rw, qm, offs, 
         quantize_piece(0, 1)
         quantize_piece(1, 0)
         quantize_piece(1, 1)
-        accs0 = grad_products(0)
-        centred = {(0, 0): centre(0, accs0, 0)}
+        accs0 = score_products(0)
+        weights = {(0, 0): weigh(0, accs0, 0)}
         for u in range(2):
             deal_piece(vcopy, 2, u)
         quantize_piece(2, 0)
         quantize_piece(2, 1)
-        centred[0, 1] = centre(0, accs0, 1)
+        weights[0, 1] = weigh(0, accs0, 1)
         for u in range(2):
             deal_piece(vcopy, 3, u)
         for u in range(2):
             quantize_piece(3, u)
-        accs1 = grad_products(1)
+        accs1 = score_products(1)
         qm0_grouped = [sb("qm0_grouped%d" % g, [P, P * PACK], BF16) for g in range(GROUPS)]
-        centred[1, 0] = centre(1, accs1, 0)
-        centred[1, 1] = centre(1, accs1, 1)
+        weights[1, 0] = weigh(1, accs1, 0)
+        weights[1, 1] = weigh(1, accs1, 1)
 
         ds_grouped = {}
 
         def multiply(name, weights, centred, tag=None):
-            ds_grouped[name] = sb(name, [P, weights.shape[2] * PACK], BF16, "k_grouped" if name == "ds_grouped0_0" else None)
+            ds_grouped[name] = sb(name, [P, weights.shape[2] * PACK], BF16, "v_grouped" if name == "ds_grouped0_0" else None)
             nc.vector.tensor_tensor(
                 out=ds_grouped[name][:].rearrange("p (c x t) -> p c t x", x=2, t=PACK),
                 in0=weights.rearrange("p t (c x) -> p c t x", x=2),
@@ -260,7 +264,7 @@ def tile_attend_gat_lse_k_kernel(tc, qT, kT, vT, doT, lse, delta, rw, qm, offs, 
             quantize(ds_mx[g], h * HALF, (h + 1) * HALF, ds_grouped["ds_grouped%d_%d" % (g, h)][:], E5M2)
 
         def multiply_ds(g, h):
-            multiply("ds_grouped%d_%d" % (g, h), weights[g][:, :, h * HALF : (h + 1) * HALF], centred[g, h][:])
+            multiply("ds_grouped%d_%d" % (g, h), weights[g, h][:], centred[g][:, :, h * HALF : (h + 1) * HALF])
 
         weave(vcopy, qm0_grouped[0][:], qm_first[0], 0, PACK)
         multiply_ds(0, 0)
@@ -275,6 +279,7 @@ def tile_attend_gat_lse_k_kernel(tc, qT, kT, vT, doT, lse, delta, rw, qm, offs, 
         weave_qm(1, (scopy, scopy))
         quantize_qm(1, "ds_grouped1_0")
         quantize_ds(1, 1)
+
 
         def finish(k, tag=None):
             acc = bank("grad", [P, N])
@@ -292,15 +297,16 @@ def tile_attend_gat_lse_k_kernel(tc, qT, kT, vT, doT, lse, delta, rw, qm, offs, 
             product(early[:], qm_mx[0], g * P, E4M3, grad_mx, lo, lo + N, E5M2, g == 0, g == GROUPS - 1)
             product(late[:], qm_mx[0], g * P, E4M3, ds_mx[g], 0, N, E5M2, g == 0, g == GROUPS - 1)
         for h, acc in enumerate((early, late)):
-            staged = sb("staged0_%d" % h, [P, HALF], F32, ("staged0_0", "staged0")[h])
+            staged = sb("staged0_%d" % h, [P, HALF], F32)
             nc.scalar.copy(out=staged[:], in_=acc[:, HALF:N])
+            if h == 0:
+                weave_qm(2, (scopy, scopy), "ds_grouped0_1")
             vcopy(windows[0][:].indirect(offsets[:, h * HALF // 16 : (h + 1) * HALF // 16]), staged[:])
             if h == 0:
-                weave_qm(2, (scopy, vcopy), "ds_grouped0_1")
+                quantize_qm(2)
         nc.sync.dma_start(out=out[0:P, :], in_=windows[0][:])
-        quantize_qm(2, "staged0")
         finish(1)
-        weave_qm(3, (scopy, scopy), "ds_grouped0_1")
+        weave_qm(3, (scopy, scopy), "staged0_1")
         quantize_qm(3)
         finish(2)
         finish(3)

@@ -22,7 +22,6 @@ PASS = P * PACK
 GROUPS = R // PASS
 HALF = N // 2
 RUN = 4
-WARM_PASSES = 2
 
 
 def tile_attend_gat_lse_k_kernel(tc, qT, kT, vT, doT, lse, delta, rw, qm, offs, out):
@@ -173,9 +172,6 @@ def tile_attend_gat_lse_k_kernel(tc, qT, kT, vT, doT, lse, delta, rw, qm, offs, 
                 )
         for h in range(2):
             quantize(k_mx, h * HALF, (h + 1) * HALF, k_grouped[h][:], E4M3)
-        warm = bank("warm", [P, N])
-        for w in range(WARM_PASSES):
-            product(warm[:], k_mx, 0, E4M3, v_mx, 0, N, E4M3)
 
         q_mx = [mx_tiles("q%d" % g, PASS) for g in range(GROUPS)]
 

@@ -67,17 +67,14 @@ def tile_attend_gat_lse_k_kernel(tc, qT, kT, vT, doT, lse, delta, rw, qm, offs, 
         v_planes = load_planes("v", vT, 0, 2)
         offsets = keep.tile([P, N // 16], U16, name="offsets")
         nc.sync.dma_start(offsets[:], offs)
-        v_planes = v_planes + load_planes("v", vT, 2, PACK)
-        stat_rows = keep.tile([P, PASS], F32, name="stat_rows")
-        nc.vector.memset(stat_rows[:], 0.0)
+        stat_rows = keep.tile([3 * 8, P], F32, name="stat_rows")
         for s, vec in enumerate((lse, delta, rw)):
-            nc.sync.dma_start(
-                out=stat_rows[4 * s : P : P // GROUPS, :],
-                in_=vec.rearrange("b (g c) o -> (b g) (c o)", g=GROUPS),
-            )
+            nc.sync.dma_start(out=stat_rows[8 * s : 8 * (s + 1), :], in_=vec.rearrange("b (i c) o -> (b i) (c o)", c=P))
+        v_planes = v_planes + load_planes("v", vT, 2, PACK)
         do_raw = load_columns("do_raw", doT, 0, R)
         k_planes = load_planes("k", kT, 0, 2) + load_planes("k", kT, 2, 3) + load_planes("k", kT, 3, PACK)
-        q_raw = [load_columns("q_raw%d" % h, qT, h * HALF, (h + 1) * HALF) for h in range(2 * GROUPS)]
+        q_raw = [load_columns("q_raw%d" % h, qT, h * HALF, (h + 1) * HALF)[:] for h in range(2 * GROUPS - 1)]
+        q_last = [load_columns("q_last%d" % h, qT, R - HALF + h * P, R - HALF + (h + 1) * P) for h in range(2)]
 
         windows = []
         for k in range(D // P):
@@ -87,11 +84,18 @@ def tile_attend_gat_lse_k_kernel(tc, qT, kT, vT, doT, lse, delta, rw, qm, offs, 
 
         ident = keep.tile([P, P], F32, name="ident")
         make_identity(nc, ident[:])
+        spread = keep.tile([P, PACK, 4, 32], F32, name="spread")
+        nc.vector.memset(spread[:], 0.0)
+        for quad in range(4):
+            nc.vector.tensor_copy(out=spread[0 : 3 * 8, :, quad, :], in_=stat_rows[:].rearrange("p (i t) -> p t i", t=PACK))
         stat_bank = bank("stat_bank", [P, PACK, P])
         for t in range(PACK):
-            nc.tensor.transpose(stat_bank[:, t, :], stat_rows[:, t:PASS:PACK], ident[:])
+            nc.tensor.transpose(stat_bank[:, t, :], spread[:, t, :, :].rearrange("p q i -> p (q i)"), ident[:])
         stats = keep.tile([P, PACK, GROUPS, 3], F32, name="stats")
-        nc.vector.tensor_copy(out=stats[:], in_=stat_bank[:].rearrange("p t (g x) -> p t g x", g=GROUPS)[:, :, :, 0:12:4])
+        turned = stat_bank[:, :, 0 : 3 * 8].rearrange("p t (s g q) -> p t g s q", g=GROUPS, q=4)
+        for quad in range(4):
+            rows = slice(32 * quad, 32 * (quad + 1))
+            nc.vector.tensor_copy(out=stats[rows, :, :, :], in_=turned[rows, :, :, :, quad])
         neg_lse = keep.tile([P, PACK, GROUPS], F32, name="neg_lse")
         nc.vector.tensor_scalar(out=neg_lse[:], in0=stats[:, :, :, 0], scalar1=-1.0, scalar2=None, op0=ALU.mult)
         neg_delta_rw = keep.tile([P, PACK, GROUPS], F32, name="neg_delta_rw")
@@ -135,12 +139,9 @@ def tile_attend_gat_lse_k_kernel(tc, qT, kT, vT, doT, lse, delta, rw, qm, offs, 
             qm_rest.append(sb("qm_rest%d" % g, [P, PACK, D - P], F32, "v_planes%d" % (2 * g)))
             nc.sync.dma_start(out=qm_rest[g][:], in_=qm_rows[g][:, :, P:D])
 
-        grad_mx = mx_tiles("grad", PASS + GROUPS * N)
-        do_mx = [mx_tiles("do0", PASS), (grad_mx[0][:, 0:PASS], grad_mx[1][:, 0:PASS])]
-        ds_mx = [
-            (grad_mx[0][:, PASS + g * N : PASS + (g + 1) * N], grad_mx[1][:, PASS + g * N : PASS + (g + 1) * N])
-            for g in range(GROUPS)
-        ]
+        grad_mx = [mx_tiles("grad%d" % g, PASS + N) for g in range(GROUPS)]
+        do_mx = [(codes[:, 0:PASS], scales[:, 0:PASS]) for codes, scales in grad_mx]
+        ds_mx = [(codes[:, PASS : PASS + N], scales[:, PASS : PASS + N]) for codes, scales in grad_mx]
         centred = []
         for g in range(GROUPS):
             pairs = pair_tiles("do%d" % g)
@@ -175,22 +176,18 @@ def tile_attend_gat_lse_k_kernel(tc, qT, kT, vT, doT, lse, delta, rw, qm, offs, 
 
         q_mx = [mx_tiles("q%d" % g, PASS) for g in range(GROUPS)]
 
-        def score_products(g):
+        def score_products(g, lo, hi):
             accs = []
-            for h in range(2):
-                for u in range(2):
-                    accs.append(bank("score", [P, 2, HALF]))
-                    for e in range(2):
-                        lhs_lo = (2 * u + e) * P
-                        product(accs[-1][:, e, :], q_mx[g], lhs_lo, E4M3, k_mx, h * HALF, (h + 1) * HALF, E4M3)
+            for u in range(2):
+                accs.append(bank("score", [P, 2, hi - lo]))
+                for e in range(2):
+                    product(accs[u][:, e, :], q_mx[g], (2 * u + e) * P, E4M3, k_mx, lo, hi, E4M3)
             return accs
 
-        def weigh(g, accs, h):
-            weights = sb("weights%d_%d" % (g, h), [P, PACK, HALF], F32, "do1_pair1" if (g, h) == (0, 1) else None)
+        def weigh(g, accs, weights):
             for t in range(PACK):
                 nc.scalar.activation(
-                    out=weights[:, t, :], in_=accs[2 * h + t // 2][:, t % 2, :], func=ACT.Exp,
-                    bias=neg_lse[:, t, g : g + 1], scale=1.0,
+                    out=weights[:, t, :], in_=accs[t // 2][:, t % 2, :], func=ACT.Exp, bias=neg_lse[:, t, g : g + 1], scale=1.0
                 )
             return weights
 
@@ -198,7 +195,7 @@ def tile_attend_gat_lse_k_kernel(tc, qT, kT, vT, doT, lse, delta, rw, qm, offs, 
         dealt = [[sb("q_dealt%d_%d" % (i, u), [P, PASS], BF16, dealt_tags[i][u]) for u in range(2)] for i in range(2 * GROUPS)]
 
         def deal_piece(copy, i, u):
-            deal(copy, dealt[i][u], q_raw[i][:], 0, u)
+            deal(copy, dealt[i][u], q_raw[i], 0, u)
 
         def quantize_piece(i, u):
             for e in range(2):
@@ -213,28 +210,31 @@ def tile_attend_gat_lse_k_kernel(tc, qT, kT, vT, doT, lse, delta, rw, qm, offs, 
         quantize_piece(0, 1)
         quantize_piece(1, 0)
         quantize_piece(1, 1)
-        accs0 = score_products(0)
-        weights = {(0, 0): weigh(0, accs0, 0)}
-        for u in range(2):
-            deal_piece(vcopy, 2, u)
+        cuts0 = (0, N // 4, HALF, N)
+        accs0 = [score_products(0, cuts0[c], cuts0[c + 1]) for c in range(3)]
+        deal_piece(vcopy, 2, 0)
+        deal_piece(vcopy, 2, 1)
+        first_weights = sb("weights0_0", [P, 2, PACK, N // 4], F32)
+        for c in range(2):
+            weigh(0, accs0[c], first_weights[:, c, :, :])
         quantize_piece(2, 0)
         quantize_piece(2, 1)
-        weights[0, 1] = weigh(0, accs0, 1)
-        for u in range(2):
-            deal_piece(vcopy, 3, u)
+        weights = {(0, 1): weigh(0, accs0[2], sb("weights0_1", [P, PACK, HALF], F32, "do1_pair1"))}
+        for h in range(2):
+            for u in range(2):
+                deal(vcopy, dealt[3][u], q_last[h][:], h * P // PACK, u)
         for u in range(2):
             quantize_piece(3, u)
-        accs1 = score_products(1)
+        accs1 = [score_products(1, h * HALF, (h + 1) * HALF) for h in range(2)]
         qm0_grouped = [sb("qm0_grouped%d" % g, [P, P * PACK], BF16) for g in range(GROUPS)]
-        weights[1, 0] = weigh(1, accs1, 0)
-        weights[1, 1] = weigh(1, accs1, 1)
+        for h in range(2):
+            weights[1, h] = weigh(1, accs1[h], sb("weights1_%d" % h, [P, PACK, HALF], F32))
 
         ds_grouped = {}
 
-        def multiply(name, weights, centred, tag=None):
-            ds_grouped[name] = sb(name, [P, weights.shape[2] * PACK], BF16, "v_grouped" if name == "ds_grouped0_0" else None)
+        def multiply(grouped, weights, centred):
             nc.vector.tensor_tensor(
-                out=ds_grouped[name][:].rearrange("p (c x t) -> p c t x", x=2, t=PACK),
+                out=grouped.rearrange("p (c x t) -> p c t x", x=2, t=PACK),
                 in0=weights.rearrange("p t (c x) -> p c t x", x=2),
                 in1=centred.rearrange("p t (c x) -> p c t x", x=2),
                 op=ALU.mult,
@@ -260,21 +260,27 @@ def tile_attend_gat_lse_k_kernel(tc, qT, kT, vT, doT, lse, delta, rw, qm, offs, 
             quantize(ds_mx[g], h * HALF, (h + 1) * HALF, ds_grouped["ds_grouped%d_%d" % (g, h)][:], E5M2)
 
         def multiply_ds(g, h):
-            multiply("ds_grouped%d_%d" % (g, h), weights[g, h][:], centred[g][:, :, h * HALF : (h + 1) * HALF])
+            name = "ds_grouped%d_%d" % (g, h)
+            ds_grouped[name] = sb(name, [P, HALF * PACK], BF16)
+            multiply(ds_grouped[name][:], weights[g, h][:], centred[g][:, :, h * HALF : (h + 1) * HALF])
 
-        weave(vcopy, qm0_grouped[0][:], qm_first[0], 0, PACK)
-        multiply_ds(0, 0)
+        first = []
+        for c in range(2):
+            first.append(sb("ds_first%d" % c, [P, P * PACK], BF16, "q_last%d" % c))
+            multiply(first[c][:], first_weights[:, c, :, :], centred[0][:, :, cuts0[c] : cuts0[c + 1]])
         multiply_ds(0, 1)
-        quantize_ds(0, 0)
-        quantize(qm_mx[0], 0, P, qm0_grouped[0][:], E4M3)
+        for c in range(2):
+            quantize(ds_mx[0], cuts0[c], cuts0[c + 1], first[c][:], E5M2)
         multiply_ds(1, 0)
-        quantize_ds(0, 1)
+        weave(vcopy, qm0_grouped[0][:], qm_first[0], 0, PACK)
         quantize_ds(1, 0)
-        quantize(qm_mx[0], P, 2 * P, qm0_grouped[1][:], E4M3)
+        for g in range(GROUPS):
+            quantize(qm_mx[0], g * P, (g + 1) * P, qm0_grouped[g][:], E4M3)
         multiply_ds(1, 1)
+        quantize_ds(0, 1)
+        quantize_ds(1, 1)
         weave_qm(1, (scopy, scopy))
         quantize_qm(1, "ds_grouped1_0")
-        quantize_ds(1, 1)
 
 
         def finish(k, tag=None):
@@ -287,19 +293,21 @@ def tile_attend_gat_lse_k_kernel(tc, qT, kT, vT, doT, lse, delta, rw, qm, offs, 
             nc.sync.dma_start(out=out[k * P : (k + 1) * P, :], in_=windows[k][:])
 
         early = bank("early", [P, N])
-        late = bank("late", [P, N])
+        late = bank("late", [P, HALF])
         for g in range(GROUPS):
-            lo = PASS + g * N - HALF
-            product(early[:], qm_mx[0], g * P, E4M3, grad_mx, lo, lo + N, E5M2, g == 0, g == GROUPS - 1)
-            product(late[:], qm_mx[0], g * P, E4M3, ds_mx[g], 0, N, E5M2, g == 0, g == GROUPS - 1)
-        for h, acc in enumerate((early, late)):
-            staged = sb("staged0_%d" % h, [P, HALF], F32)
-            nc.scalar.copy(out=staged[:], in_=acc[:, HALF:N])
-            if h == 0:
-                weave_qm(2, (scopy, scopy), "ds_grouped0_1")
-            vcopy(windows[0][:].indirect(offsets[:, h * HALF // 16 : (h + 1) * HALF // 16]), staged[:])
-            if h == 0:
-                quantize_qm(2)
+            product(early[:], qm_mx[0], g * P, E4M3, grad_mx[g], PASS - HALF, PASS + HALF, E5M2, g == 0, g == GROUPS - 1)
+        for g in range(GROUPS):
+            product(late[:], qm_mx[0], g * P, E4M3, ds_mx[g], HALF, N, E5M2, g == 0, g == GROUPS - 1)
+        staged0 = []
+        for h, acc in enumerate((early[:, HALF:N], late[:])):
+            staged0.append(sb("staged0_%d" % h, [P, HALF], F32))
+            nc.scalar.copy(out=staged0[h][:], in_=acc)
+            vcopy(windows[0][:].indirect(offsets[:, h * HALF // 16 : (h + 1) * HALF // 16]), staged0[h][:])
+        qm_mx[2] = mx_tiles("qm2", GROUPS * P)
+        for g in range(GROUPS):
+            grouped = sb("qm_grouped2_%d" % g, [P, P * PACK], BF16, "qm0_codes" if g else None)
+            weave(scopy, grouped[:], qm_rest[g][:, :, P : 2 * P], 0, PACK)
+            quantize(qm_mx[2], g * P, (g + 1) * P, grouped[:], E4M3)
         nc.sync.dma_start(out=out[0:P, :], in_=windows[0][:])
         finish(1)
         weave_qm(3, (scopy, scopy), "staged0_1")

from contextlib import ExitStack

import concourse.mybir as mybir
from concourse.masks import make_identity

N, T, D, DV, R = 512, 2048, 512, 512, 1024
FLOPS = 2 * R * N * (D + DV + D)

F32 = mybir.dt.float32
BF16 = mybir.dt.bfloat16
U32 = mybir.dt.uint32
U16 = mybir.dt.uint16
U8 = mybir.dt.uint8
E4M3 = mybir.dt.float8_e4m3fn_x4
E5M2 = mybir.dt.float8_e5m2_x4
ACT = mybir.ActivationFunctionType
ALU = mybir.AluOpType

P = 128
PACK = 4
PASS = P * PACK
GROUPS = R // PASS
HALF = N // 2
RUN = 4


def tile_attend_gat_lse_k_kernel(tc, qT, kT, vT, doT, lse, delta, rw, qm, offs, out):
    nc = tc.nc
    vcopy, scopy = nc.vector.tensor_copy, nc.scalar.copy
    with ExitStack() as ctx:
        keep = ctx.enter_context(tc.tile_pool(name="keep", bufs=1))
        psum = ctx.enter_context(tc.psum_pool(name="psum", bufs=8))

        def bank(name, shape):
            return psum.tile(shape, F32, name=name, tag="bank")

        def sb(name, shape, dtype, tag=None):
            return keep.tile(shape, dtype, name=name, tag=tag or name, align_bytes=64)

        def mx_tiles(name, width, tag=None):
            return sb(name + "_codes", [P, width], U32, tag), sb(name + "_scales", [P, width], U8)

        def quantize(mx, lo, hi, grouped, fmt):
            nc.vector.quantize_mx(out=mx[0][:, lo:hi].bitcast(fmt), scales=mx[1][:, lo:hi], in_=grouped)

        def product(acc, lhs, lhs_lo, lhs_fmt, rhs, rhs_lo, rhs_hi, rhs_fmt, start=True, stop=True):
            nc.tensor.matmul_mx(
                out=acc,
                lhsT=lhs[0][:, lhs_lo : lhs_lo + P].bitcast(lhs_fmt),
                lhsT_scale=lhs[1][:, lhs_lo : lhs_lo + P],
                rhs=rhs[0][:, rhs_lo:rhs_hi].bitcast(rhs_fmt),
                rhs_scale=rhs[1][:, rhs_lo:rhs_hi],
                start=start,
                stop=stop,
            )

        def load_planes(name, pool, lo, hi):
            piece = sb("%s_planes%d" % (name, lo), [P, hi - lo, T], F32)
            nc.sync.dma_start(out=piece[:], in_=pool.rearrange("(p j) t -> p j t", j=PACK)[:, lo:hi, :])
            return [piece[:, j, :] for j in range(hi - lo)]

        def load_columns(name, src, lo, hi, tag=None):
            piece = sb(name, [P, PACK, hi - lo], F32, tag)
            nc.sync.dma_start(out=piece[:], in_=src[0].rearrange("(p j) r -> p j r", j=PACK)[:, :, lo:hi])
            return piece

        v_planes = load_planes("v", vT, 0, 2)
        offsets = keep.tile([P, N // 16], U16, name="offsets")
        nc.sync.dma_start(offsets[:], offs)
        stat_rows = keep.tile([3 * 8, P], F32, name="stat_rows")
        for s, vec in enumerate((lse, delta, rw)):
            nc.sync.dma_start(out=stat_rows[8 * s : 8 * (s + 1), :], in_=vec.rearrange("b (i c) o -> (b i) (c o)", c=P))
        v_planes = v_planes + load_planes("v", vT, 2, PACK)
        do_raw = load_columns("do_raw", doT, 0, R)
        k_planes = load_planes("k", kT, 0, 2) + load_planes("k", kT, 2, 3) + load_planes("k", kT, 3, PACK)
        q_raw = [load_columns("q_raw%d" % h, qT, h * HALF, (h + 1) * HALF)[:] for h in range(2 * GROUPS - 1)]
        q_last = [load_columns("q_last%d" % h, qT, R - HALF + h * P, R - HALF + (h + 1) * P) for h in range(2)]

        windows = []
        for k in range(D // P):
            window = keep.tile([P, T], F32, name="window%d" % k)
            (nc.vector if k == 0 else nc.gpsimd).memset(window[:], 0.0)
            windows.append(window)

        ident = keep.tile([P, P], F32, name="ident")
        make_identity(nc, ident[:])
        spread = keep.tile([P, PACK, 4, 32], F32, name="spread")
        nc.vector.memset(spread[:], 0.0)
        for quad in range(4):
            nc.vector.tensor_copy(out=spread[0 : 3 * 8, :, quad, :], in_=stat_rows[:].rearrange("p (i t) -> p t i", t=PACK))
        stat_bank = bank("stat_bank", [P, PACK, P])
        for t in range(PACK):
            nc.tensor.transpose(stat_bank[:, t, :], spread[:, t, :, :].rearrange("p q i -> p (q i)"), ident[:])
        stats = keep.tile([P, PACK, GROUPS, 3], F32, name="stats")
        turned = stat_bank[:, :, 0 : 3 * 8].rearrange("p t (s g q) -> p t g s q", g=GROUPS, q=4)
        for quad in range(4):
            rows = slice(32 * quad, 32 * (quad + 1))
            nc.vector.tensor_copy(out=stats[rows, :, :, :], in_=turned[rows, :, :, :, quad])
        neg_lse = keep.tile([P, PACK, GROUPS], F32, name="neg_lse")
        nc.vector.tensor_scalar(out=neg_lse[:], in0=stats[:, :, :, 0], scalar1=-1.0, scalar2=None, op0=ALU.mult)
        neg_delta_rw = keep.tile([P, PACK, GROUPS], F32, name="neg_delta_rw")
        nc.vector.scalar_tensor_tensor(
            out=neg_delta_rw[:], in0=stats[:, :, :, 1], scalar=-1.0, in1=stats[:, :, :, 2], op0=ALU.mult, op1=ALU.mult
        )

        def weave(copy, grouped, planes, j0, j1):
            copy(
                out=grouped.rearrange("p (c x j) -> p c j x", x=RUN, j=PACK)[:, :, j0:j1, :],
                in_=planes[:, j0:j1, :].rearrange("p j (c x) -> p c j x", x=RUN),
            )

        def deal(copy, pair, raw, m0, u):
            width = raw.shape[2] // PACK
            copy(
                out=pair[:].rearrange("p (t m j) -> p m j t", t=2, j=PACK)[:, m0 : m0 + width, :, :],
                in_=raw.rearrange("p j (m t) -> p m j t", t=PACK)[:, :, :, 2 * u : 2 * u + 2],
            )

        def pair_tiles(name, tag=None):
            return [sb("%s_pair%d" % (name, u), [P, 2 * PASS], BF16, tag and "%s_pair%d" % (tag, u)) for u in range(2)]

        def quantize_pair(mx, pairs, u, fmt):
            quantize(mx, 2 * P * u, 2 * P * (u + 1), pairs[u][:], fmt)

        v_picked = sb("v_picked", [P, PACK, N], F32)
        for j in range(PACK):
            vcopy(v_picked[:, j, :], v_planes[j].indirect(offsets[:]))
        v_grouped = sb("v_grouped", [P, N * PACK], BF16)
        weave(vcopy, v_grouped[:], v_picked, 0, PACK)
        v_mx = mx_tiles("v", N)
        quantize(v_mx, 0, N, v_grouped[:], E4M3)

        qm_rows = [qm[0, g * PASS : (g + 1) * PASS, :].rearrange("(p t) d -> p t d", t=PACK) for g in range(GROUPS)]
        qm_first, qm_rest = [], []
        for g in range(GROUPS):
            qm_first.append(sb("qm_first%d" % g, [P, PACK, P], F32))
            nc.sync.dma_start(out=qm_first[g][:], in_=qm_rows[g][:, :, 0:P])
        for g in range(GROUPS):
            qm_rest.append(sb("qm_rest%d" % g, [P, PACK, D - P], F32, "v_planes%d" % (2 * g)))
            nc.sync.dma_start(out=qm_rest[g][:], in_=qm_rows[g][:, :, P:D])

        grad_mx = [mx_tiles("grad%d" % g, PASS + N) for g in range(GROUPS)]
        do_mx = [(codes[:, 0:PASS], scales[:, 0:PASS]) for codes, scales in grad_mx]
        ds_mx = [(codes[:, PASS : PASS + N], scales[:, PASS : PASS + N]) for codes, scales in grad_mx]
        centred = []
        for g in range(GROUPS):
            pairs = pair_tiles("do%d" % g)
            for u in range(2):
                deal(vcopy, pairs[u], do_raw[:, :, g * PASS : (g + 1) * PASS], 0, u)
            for u in range(2):
                quantize_pair(do_mx[g], pairs, u, E5M2)
            centred.append(sb("centred%d" % g, [P, PACK, N], F32))
            for t in range(PACK):
                acc = bank("dp", [P, N])
                product(acc[:], do_mx[g], t * P, E5M2, v_mx, 0, N, E4M3)
                nc.scalar.activation(
                    out=centred[g][:, t, :], in_=acc[:], func=ACT.Identity,
                    bias=neg_delta_rw[:, t, g : g + 1], scale=stats[:, t, g, 2:3],
                )

        k_picked = sb("k_picked", [P, 2, N], F32, "v_picked")
        k_grouped = [sb("k_grouped%d" % h, [P, HALF * PACK], BF16) for h in range(2)]
        k_mx = mx_tiles("k", N)
        for j in range(2):
            vcopy(k_picked[:, j, :], k_planes[j].indirect(offsets[:]))
        for h in range(2):
            weave(scopy, k_grouped[h][:], k_picked[:, :, h * HALF : (h + 1) * HALF], 0, 2)
        for j in range(2, PACK):
            for h in range(2):
                vcopy(
                    k_grouped[h][:].rearrange("p (s j) -> p s j", j=PACK)[:, :, j],
                    k_planes[j].indirect(offsets[:, h * HALF // 16 : (h + 1) * HALF // 16]),
                )
        for h in range(2):
            quantize(k_mx, h * HALF, (h + 1) * HALF, k_grouped[h][:], E4M3)

        q_mx = [mx_tiles("q%d" % g, PASS) for g in range(GROUPS)]

        def score_products(g, lo, hi):
            accs = []
            for u in range(2):
                accs.append(bank("score", [P, 2, hi - lo]))
                for e in range(2):
                    product(accs[u][:, e, :], q_mx[g], (2 * u + e) * P, E4M3, k_mx, lo, hi, E4M3)
            return accs

        def weigh(g, accs, weights):
            for t in range(PACK):
                nc.scalar.activation(
                    out=weights[:, t, :], in_=accs[t // 2][:, t % 2, :], func=ACT.Exp, bias=neg_lse[:, t, g : g + 1], scale=1.0
                )
            return weights

        dealt_tags = (("do0_pair0", "do0_pair1"), (None, None), ("do1_pair0", "do1_pair1"), (None, None))
        dealt = [[sb("q_dealt%d_%d" % (i, u), [P, PASS], BF16, dealt_tags[i][u]) for u in range(2)] for i in range(2 * GROUPS)]

        def deal_piece(copy, i, u):
            deal(copy, dealt[i][u], q_raw[i], 0, u)

        def quantize_piece(i, u):
            for e in range(2):
                lo = (2 * u + e) * P + (i % 2) * P // 2
                quantize(q_mx[i // 2], lo, lo + P // 2, dealt[i][u][:, e * HALF : (e + 1) * HALF], E4M3)

        deal_piece(scopy, 0, 0)
        deal_piece(scopy, 0, 1)
        quantize_piece(0, 0)
        deal_piece(vcopy, 1, 0)
        deal_piece(scopy, 1, 1)
        quantize_piece(0, 1)
        quantize_piece(1, 0)
        quantize_piece(1, 1)
        cuts0 = (0, N // 4, HALF, N)
        accs0 = [score_products(0, cuts0[c], cuts0[c + 1]) for c in range(3)]
        deal_piece(vcopy, 2, 0)
        deal_piece(vcopy, 2, 1)
        first_weights = sb("weights0_0", [P, 2, PACK, N // 4], F32)
        for c in range(2):
            weigh(0, accs0[c], first_weights[:, c, :, :])
        quantize_piece(2, 0)
        quantize_piece(2, 1)
        weights = {(0, 1): weigh(0, accs0[2], sb("weights0_1", [P, PACK, HALF], F32, "do1_pair1"))}
        for h in range(2):
            for u in range(2):
                deal(vcopy, dealt[3][u], q_last[h][:], h * P // PACK, u)
        for u in range(2):
            quantize_piece(3, u)
        accs1 = [score_products(1, h * HALF, (h + 1) * HALF) for h in range(2)]
        qm0_grouped = [sb("qm0_grouped%d" % g, [P, P * PACK], BF16) for g in range(GROUPS)]
        for h in range(2):
            weights[1, h] = weigh(1, accs1[h], sb("weights1_%d" % h, [P, PACK, HALF], F32))

        ds_grouped = {}

        def multiply(grouped, weights, centred):
            nc.vector.tensor_tensor(
                out=grouped.rearrange("p (c x t) -> p c t x", x=2, t=PACK),
                in0=weights.rearrange("p t (c x) -> p c t x", x=2),
                in1=centred.rearrange("p t (c x) -> p c t x", x=2),
                op=ALU.mult,
            )

        qm_mx = [None] * (D // P)
        qm_grouped = [None] * (D // P)

        def weave_qm(k, copies, tag=None):
            qm_grouped[k] = sb("qm_grouped%d" % k, [P, GROUPS, P * PACK], BF16, tag)
            for g in range(GROUPS):
                rows = qm_rest[g][:, :, (k - 1) * P : k * P]
                weave(copies[g], qm_grouped[k][:, g, :], rows, 0, PACK)

        def quantize_qm(k, tag=None):
            qm_mx[k] = mx_tiles("qm%d" % k, GROUPS * P, tag)
            quantize(qm_mx[k], 0, GROUPS * P, qm_grouped[k][:].rearrange("p g w -> p (g w)"), E4M3)

        qm_mx[0] = mx_tiles("qm0", GROUPS * P)
        weave(scopy, qm0_grouped[1][:], qm_first[1], 0, PACK)

        def quantize_ds(g, h):
            quantize(ds_mx[g], h * HALF, (h + 1) * HALF, ds_grouped["ds_grouped%d_%d" % (g, h)][:], E5M2)

        def multiply_ds(g, h):
            name = "ds_grouped%d_%d" % (g, h)
            ds_grouped[name] = sb(name, [P, HALF * PACK], BF16)
            multiply(ds_grouped[name][:], weights[g, h][:], centred[g][:, :, h * HALF : (h + 1) * HALF])

        first = []
        for c in range(2):
            first.append(sb("ds_first%d" % c, [P, P * PACK], BF16, "q_last%d" % c))
            multiply(first[c][:], first_weights[:, c, :, :], centred[0][:, :, cuts0[c] : cuts0[c + 1]])
        multiply_ds(0, 1)
        for c in range(2):
            quantize(ds_mx[0], cuts0[c], cuts0[c + 1], first[c][:], E5M2)
        multiply_ds(1, 0)
        weave(vcopy, qm0_grouped[0][:], qm_first[0], 0, PACK)
        quantize_ds(1, 0)
        for g in range(GROUPS):
            quantize(qm_mx[0], g * P, (g + 1) * P, qm0_grouped[g][:], E4M3)
        multiply_ds(1, 1)
        quantize_ds(0, 1)
        quantize_ds(1, 1)
        weave_qm(1, (scopy, scopy))
        quantize_qm(1, "ds_grouped1_0")


        def finish(k, tag=None):
            acc = bank("grad", [P, N])
            for g in reversed(range(GROUPS)):
                product(acc[:], qm_mx[k], g * P, E4M3, ds_mx[g], 0, N, E5M2, g == GROUPS - 1, g == 0)
            staged = sb("staged%d" % k, [P, N], F32, tag)
            nc.scalar.copy(out=staged[:], in_=acc[:])
            vcopy(windows[k][:].indirect(offsets[:]), staged[:])
            nc.sync.dma_start(out=out[k * P : (k + 1) * P, :], in_=windows[k][:])

        early = bank("early", [P, N])
        late = bank("late", [P, HALF])
        for g in range(GROUPS):
            product(early[:], qm_mx[0], g * P, E4M3, grad_mx[g], PASS - HALF, PASS + HALF, E5M2, g == 0, g == GROUPS - 1)
        for g in range(GROUPS):
            product(late[:], qm_mx[0], g * P, E4M3, ds_mx[g], HALF, N, E5M2, g == 0, g == GROUPS - 1)
        staged0 = []
        for h, acc in enumerate((early[:, HALF:N], late[:])):
            staged0.append(sb("staged0_%d" % h, [P, HALF], F32))
            nc.scalar.copy(out=staged0[h][:], in_=acc)
            vcopy(windows[0][:].indirect(offsets[:, h * HALF // 16 : (h + 1) * HALF // 16]), staged0[h][:])
        qm_mx[2] = mx_tiles("qm2", GROUPS * P)
        for g in range(GROUPS):
            grouped = sb("qm_grouped2_%d" % g, [P, P * PACK], BF16, "qm0_codes" if g else None)
            weave(scopy, grouped[:], qm_rest[g][:, :, P : 2 * P], 0, PACK)
            quantize(qm_mx[2], g * P, (g + 1) * P, grouped[:], E4M3)
        nc.sync.dma_start(out=out[0:P, :], in_=windows[0][:])
        finish(1)
        weave_qm(3, (scopy, scopy), "staged0_1")
        quantize_qm(3)
        finish(2)
        finish(3)
